import numpy as np
import ml_dtypes


def mxq(x, axis, fmt="e4m3"):
    dtype, down = {"e4m3": (ml_dtypes.float8_e4m3fn, 7), "e5m2": (ml_dtypes.float8_e5m2, 14)}[fmt]
    v = np.moveaxis(np.asarray(x, np.float32).astype(ml_dtypes.bfloat16).astype(np.float64), axis, -1)
    blocks = v.reshape(v.shape[:-1] + (-1, 32))
    amax = np.abs(blocks).max(-1, keepdims=True)
    byte = np.maximum(np.where(amax > 0, np.frexp(amax)[1] - 1 + 127, 0) - down, 1)
    scale = np.exp2(byte - 127.0)
    codes = (blocks / scale).astype(np.float32).astype(dtype).astype(np.float64)
    return np.moveaxis((codes * scale).reshape(v.shape), -1, axis)


WIDE = False


def mx_kscale(k):
    if not WIDE:
        return np.ones(k)
    levels = np.array([10, -10, 5, -5, 0])
    if k % 512:
        return np.exp2(np.random.permutation(np.resize(levels, k // 32))).repeat(32)
    a = np.empty((k // 512, 16))
    for p in range(k // 512):
        a[p, :8] = np.random.permutation(np.resize(levels, 8))
        for g in range(8):
            far = levels[np.abs(levels - a[p, g]) >= 10]
            a[p, g + 8] = far[np.random.randint(len(far))]
    return np.exp2(a.ravel()).repeat(32)


BF16 = ml_dtypes.bfloat16


def bf(x):
    return np.asarray(x, np.float32).astype(BF16)


def f64(x):
    return np.asarray(x).astype(np.float64)


M, K, N = 1024, 512, 1536

SLOPE = 0.2


def leaky(z):
    return np.maximum(z, SLOPE * z)


def draw0():
    s, t, u = mx_kscale(K), mx_kscale(N), mx_kscale(M)
    return {"x": bf(np.random.standard_normal((M, K)) * s),
            "w": bf(np.random.standard_normal((K, N)) / np.sqrt(K) / s[:, None]),
            "b": bf(0.3 * np.random.standard_normal(N)),
            "fgain": bf((1 + 0.1 * np.random.standard_normal(N)) * t),
            "sweight": bf(np.exp(0.3 * np.random.standard_normal(M)) * u),
            "p": bf(np.random.standard_normal((N, N)) / np.sqrt(N) / t[:, None]),
            "q": bf(np.random.standard_normal((M, M)) / np.sqrt(M) / u),
            "pgain": bf(1 + 0.1 * np.random.standard_normal(N)),
            "cgain": bf((1 + 0.1 * np.random.standard_normal(N)) / t),
            "cbias": bf(0.3 * np.random.standard_normal(N))}


def core(x, w, b, fgain, sweight, p, q, pgain, cgain, cbias):
    z = mxq(f64(x), 1, "e4m3") @ mxq(f64(w), 0, "e4m3")
    h = leaky(z + f64(b)) * f64(fgain) * f64(sweight)[:, None]
    a = mxq(h, 1, "e4m3") @ mxq(f64(p), 0, "e4m3")
    own = a / np.sqrt(np.mean(a * a, axis=1, keepdims=True)) * f64(pgain)
    c = mxq(f64(q), 1, "e4m3") @ mxq(h, 0, "e4m3")
    ctx = c * f64(cgain) + f64(cbias)
    closeness = np.exp(-np.abs(own - ctx))
    return own, closeness


def e4m3fn_bytes(y):
    return np.clip(np.asarray(y, np.float64), -448.0, 448.0).astype(np.float32).astype(ml_dtypes.float8_e4m3fn).view(np.uint8)


def e4m3fn_values(b):
    return np.asarray(b, np.uint8).view(ml_dtypes.float8_e4m3fn).astype(np.float64)


def setup_inputs():
    d = draw0()
    x0 = np.asarray(d['p']).astype(np.float64)
    s = (np.max(np.abs(x0), axis=(1,), keepdims=True) / 448.0).astype(np.float32)
    out = {}
    for k, v in d.items():
        if k == 'p':
            out['p_bytes'] = e4m3fn_bytes(x0 / s.astype(np.float64))
            out['p_scale'] = s
        else:
            out[k] = v
    return out


def reference(x, w, b, fgain, sweight, p_bytes, p_scale, q, pgain, cgain, cbias):
    return core(x, w, b, fgain, sweight, e4m3fn_values(p_bytes) * p_scale.astype(np.float64), q, pgain, cgain, cbias)

@@ -1,0 +1,514 @@
+from contextlib import ExitStack
+
+import concourse.mybir as mybir
+from concourse.masks import make_identity
+
+M, K, N = 1024, 512, 1536
+FLOPS = 2 * M * N * (K + N + M)
+
+F32 = mybir.dt.float32
+BF16 = mybir.dt.bfloat16
+U32 = mybir.dt.uint32
+U8 = mybir.dt.uint8
+FP8 = mybir.dt.float8_e4m3fn
+FP8X4 = mybir.dt.float8_e4m3fn_x4
+ALU = mybir.AluOpType
+ACT = mybir.ActivationFunctionType
+
+P = 128
+SLOPE = 0.2
+
+FILL = {
+    0: [('xh', ())],
+    1: [('xq', ()), ('pw', (0, 0)), ('pw', (0, 2))],
+    2: [('pm', (0, 0)), ('pm', (0, 1))],
+    3: [('wi', (1,)), ('tr', (0, 0)), ('pe', (0, 0)), ('pe', (0, 1)), ('pw', (1, 0)), ('pw', (1, 2))],
+    4: [('wq', (1,)), ('ev', (0, 0)), ('pq', (0,)), ('pm', (1, 0)), ('pm', (1, 1))],
+    5: [('il', (0,)), ('tr', (0, 1)), ('qt', (0, 0)), ('pe', (1, 0)), ('pe', (1, 1)), ('pw', (2, 0)), ('pw', (2, 2))],
+    6: [('qa', (0,)), ('ev', (0, 1)), ('qe', (0, 0)), ('qt', (0, 1)), ('pq', (1,)), ('pm', (2, 0)), ('pm', (2, 1))],
+    7: [('qc', (0,)), ('tr', (1, 0)), ('qe', (0, 1)), ('qt', (0, 2)), ('pe', (2, 0)), ('pe', (2, 1))],
+    8: [('ev', (1, 0)), ('qe', (0, 2)), ('qt', (0, 3)), ('pq', (2,)), ('pw', (3, 0)), ('pw', (3, 2))],
+    9: [('il', (1,)), ('tr', (1, 1)), ('qe', (0, 3)), ('pm', (3, 0)), ('pm', (3, 1))],
+    10: [('wi', (2,)), ('qa', (1,)), ('ev', (1, 1)), ('qq', (0,)), ('pe', (3, 0)), ('pe', (3, 1))],
+    11: [('wq', (2,)), ('qc', (1,)), ('tr', (2, 0)), ('qt', (1, 0)), ('pq', (3,)), ('pw', (4, 0)), ('pw', (4, 2))],
+    12: [('ev', (2, 0)), ('qe', (1, 0)), ('qt', (1, 1)), ('pg', (0,)), ('pm', (4, 0)), ('pm', (4, 1))],
+    13: [('il', (2,)), ('tr', (2, 1)), ('qe', (1, 1)), ('qt', (1, 2)), ('pg', (1,)), ('pe', (4, 0)), ('pe', (4, 1)), ('pw', (5, 0)), ('pw', (5, 2))],
+    14: [('qa', (2,)), ('ev', (2, 1)), ('qe', (1, 2)), ('qt', (1, 3)), ('pg', (2,)), ('pq', (4,)), ('pm', (5, 0)), ('pm', (5, 1))],
+    15: [('qc', (2,)), ('tr', (3, 0)), ('qe', (1, 3)), ('pe', (5, 0)), ('pe', (5, 1)), ('pw', (6, 0)), ('pw', (6, 2))],
+    16: [('ev', (3, 0)), ('qq', (1,)), ('pq', (5,)), ('pm', (6, 0)), ('pm', (6, 1))],
+    17: [('il', (3,)), ('tr', (3, 1)), ('pe', (6, 0)), ('pe', (6, 1)), ('pw', (7, 0)), ('pw', (7, 2)), ('cm', (0, 0, 0)), ('ce', (0, 0, 0)), ('cm', (0, 0, 1)), ('ce', (0, 0, 1))],
+    18: [('qa', (3,)), ('ev', (3, 1)), ('pq', (6,)), ('pm', (7, 0)), ('pm', (7, 1)), ('cm', (0, 0, 2)), ('ce', (0, 0, 2)), ('cm', (0, 0, 3)), ('ce', (0, 0, 3))],
+    19: [('qc', (3,)), ('tr', (4, 0)), ('pe', (7, 0)), ('pe', (7, 1)), ('pw', (8, 0)), ('pw', (8, 2)), ('cm', (0, 1, 0)), ('ce', (0, 1, 0)), ('cm', (0, 1, 1)), ('ce', (0, 1, 1))],
+    20: [('ev', (4, 0)), ('pq', (7,)), ('pm', (8, 0)), ('pm', (8, 1)), ('cm', (0, 1, 2)), ('ce', (0, 1, 2)), ('cm', (0, 1, 3)), ('ce', (0, 1, 3))],
+    21: [('il', (4,)), ('tr', (4, 1)), ('pe', (8, 0)), ('pe', (8, 1)), ('cm', (1, 0, 0)), ('ce', (1, 0, 0)), ('cm', (1, 0, 1)), ('ce', (1, 0, 1))],
+    22: [('qa', (4,)), ('ev', (4, 1)), ('pq', (8,)), ('cm', (1, 0, 2)), ('ce', (1, 0, 2)), ('cm', (1, 0, 3)), ('ce', (1, 0, 3))],
+    23: [('qc', (4,)), ('tr', (5, 0)), ('cm', (1, 1, 0)), ('ce', (1, 1, 0)), ('cm', (1, 1, 1)), ('ce', (1, 1, 1))],
+    24: [('ev', (5, 0)), ('cm', (1, 1, 2)), ('ce', (1, 1, 2)), ('cm', (1, 1, 3)), ('ce', (1, 1, 3))],
+    25: [('il', (5,)), ('tr', (5, 1))],
+    26: [('qa', (5,)), ('ev', (5, 1))],
+    27: [('qc', (5,))],
+}
+SLOTS = 28
+GRP_BUFS = 5
+WIDEN_S = {1, 3, 5, 7}
+VABS = [512, 512, 512, 512, 512, 512, 512, 512]
+
+
+def tile_minibatch_discriminator_features_f6_kernel(
+    tc, x, w, b, fgain, sweight, p_bytes, p_scale, q, pgain, cgain, cbias, own_out, close_out
+):
+    nc = tc.nc
+    with ExitStack() as ctx:
+        const = ctx.enter_context(tc.tile_pool(name="const", bufs=1))
+        codes = ctx.enter_context(tc.tile_pool(name="codes", bufs=1))
+        grp_pool = ctx.enter_context(tc.tile_pool(name="grp", bufs=GRP_BUFS))
+        pw_pool = ctx.enter_context(tc.tile_pool(name="pw", bufs=2))
+        ht_pool = ctx.enter_context(tc.tile_pool(name="ht", bufs=3))
+        ul_pool = ctx.enter_context(tc.tile_pool(name="ul", bufs=3))
+        small = ctx.enter_context(tc.tile_pool(name="small", bufs=4))
+        ctxt_pool = ctx.enter_context(tc.tile_pool(name="ctxt", bufs=1))
+        psum = ctx.enter_context(tc.psum_pool(name="psum", bufs=8))
+
+        ident = const.tile([P, P], F32, name="ident")
+        make_identity(nc, ident[:])
+        ident_b = const.tile([P, P], BF16, name="ident_b")
+
+        def code_pair(name, width):
+            c = codes.tile([P, width], U32, name=name + "_c", align_bytes=64)
+            s = codes.tile([P, width], U8, name=name + "_s", align_bytes=64)
+            return c, s
+
+        def quant(pair, lo, hi, src):
+            nc.vector.quantize_mx(out=pair[0][:, lo:hi].bitcast(FP8X4), scales=pair[1][:, lo:hi], in_=src)
+
+        def mm(out, lhs, l0, rhs, r0, n, start, stop):
+            nc.tensor.matmul_mx(
+                out=out,
+                lhsT=lhs[0][:, l0 : l0 + P].bitcast(FP8X4),
+                lhsT_scale=lhs[1][:, l0 : l0 + P],
+                rhs=rhs[0][:, r0 : r0 + n].bitcast(FP8X4),
+                rhs_scale=rhs[1][:, r0 : r0 + n],
+                start=start,
+                stop=stop,
+            )
+
+        def bank(shape, dtype=F32):
+            return psum.tile(shape, dtype, name="bank", tag="bank")
+
+        def flat(t):
+            return t[:].rearrange("p m t -> p (m t)")
+
+        def group_tile():
+            return grp_pool.tile([P, 512, 4], BF16, name="grp", tag="grp", align_bytes=64)
+
+        xq = [code_pair("xq%d" % i, 512) for i in range(2)]
+        wq = [code_pair("wq%d" % i, 512) for i in range(3)]
+        ha = [code_pair("ha%d" % i, 1024) for i in range(3)]
+        hc = [code_pair("hc%d" % i, 1536) for i in range(2)]
+        qq = [code_pair("qq%d" % i, 1024) for i in range(2)]
+        pq = [code_pair("pq%d" % i, 1536) for i in range(3)]
+
+        with tc.manual_schedule():
+            with tc.tile_pool(name="raw", bufs=1) as raw, tc.tile_pool(name="raw4", bufs=6) as raw4:
+                warm = const.tile([P, 1], F32, name="warm")
+                mhalf = const.tile([P, 1], F32, name="mhalf")
+                vrows = const.tile([P, 512], BF16, name="vrows")
+                rows = raw.tile([P, 2560], BF16, name="rows")
+                ones = const.tile([P, P], BF16, name="ones")
+                nc.vector.memset(warm[:], 0.0)
+                nc.vector.memset(vrows[:], 0.0)
+                nc.vector.memset(rows[:], 0.0)
+                nc.vector.memset(ones[:], 1.0)
+                nc.vector.memset(mhalf[:], -0.5)
+
+                xv = x.rearrange("(h r p) k -> h p r k", p=P, r=4)
+                wv = w.rearrange("(p j) (g c) -> g p j c", j=4, g=3)
+                qv = q.rearrange("(s r p) k -> s p r k", p=P, r=2)
+                pv = p_bytes.rearrange("(g p t) n -> g p t n", p=P, t=4)
+                p_raw = [raw.tile([P, 4, N], U8, name="p_raw%d" % i) for i in range(3)]
+                p_sc = const.tile([P, 3, 4], F32, name="p_sc")
+                x_raw, w_raw, q_raw = {}, {}, {}
+
+                def load4(store, i, shape, src):
+                    store[i] = raw4.tile(shape, BF16, name="raw4", tag="raw4")
+                    nc.sync.dma_start(out=store[i][:], in_=src)
+
+                def load_p(g):
+                    for i in range(2):
+                        nc.sync.dma_start(out=p_raw[g][:, 2 * i : 2 * i + 2, :], in_=pv[g][:, 2 * i : 2 * i + 2, :])
+
+                for v, vec in enumerate((b, fgain, cgain, cbias)):
+                    nc.scalar.dma_start(out=vrows[3 * v : 3 * v + 3, :], in_=vec.rearrange("(g c) -> g c", g=3))
+                nc.scalar.dma_start(out=rows[0:1, 0:M], in_=sweight.rearrange("(o m) -> o m", o=1))
+                nc.scalar.dma_start(out=rows[0:1, M : M + N], in_=pgain.rearrange("(o m) -> o m", o=1))
+                load4(x_raw, 0, [P, 4, K], xv[0])
+                load4(w_raw, 0, [P, 4, 512], wv[0])
+                load4(x_raw, 1, [P, 4, K], xv[1])
+                nc.sync.dma_start(out=p_sc[:], in_=p_scale.rearrange("(g p t) o -> p g (t o)", p=P, t=4))
+                load_p(0)
+                load4(w_raw, 1, [P, 4, 512], wv[1])
+                load4(q_raw, 0, [P, 2, M], qv[0])
+                load4(q_raw, 1, [P, 2, M], qv[1])
+                load4(w_raw, 2, [P, 4, 512], wv[2])
+                load_p(1)
+                load4(q_raw, 2, [P, 2, M], qv[2])
+                load4(q_raw, 3, [P, 2, M], qv[3])
+                load_p(2)
+
+                nc.scalar.activation(out=warm[:], in_=warm[:], func=ACT.Exp)
+
+                gx = {}
+
+                def x_half(h):
+                    gx[h] = group_tile()
+                    gw = flat(gx[h]).bitcast(F32).rearrange("p (r m u) -> p r m u", r=4, u=2)
+                    for i in range(2):
+                        tb = bank([P, 2, 2, P])
+                        for r in range(2):
+                            words = x_raw[h][:, 2 * i + r, :].bitcast(F32)
+                            for u in range(2):
+                                nc.tensor.transpose(tb[:, r, u, :], words[:, u::2], ident[:])
+                        src = tb[:].rearrange("p r u m -> p r m u")
+                        if i == 0:
+                            nc.vector.tensor_copy(out=gw[:, 2 * i : 2 * i + 2], in_=src)
+                        else:
+                            nc.scalar.copy(out=gw[:, 2 * i : 2 * i + 2], in_=src)
+
+                def x_quant(h):
+                    quant(xq[h], 0, 512, flat(gx[h]))
+
+                gw_ = {}
+
+                def w_il(g):
+                    gw_[g] = group_tile()
+                    nc.vector.tensor_copy(
+                        out=gw_[g][:].rearrange("p (t m) j -> p t m j", t=4),
+                        in_=w_raw[g][:].rearrange("p j (m t) -> p t m j", t=4),
+                    )
+
+                def w_quant(g):
+                    quant(wq[g], 0, 512, flat(gw_[g]))
+
+                cols = const.tile([P, 4, 3, 4], F32, name="cols")
+                b_s = const.tile([P, 3, 4], F32, name="b_s")
+
+                def columns():
+                    vbank = bank([P, 2, P])
+                    for u in range(2):
+                        nc.tensor.transpose(vbank[:, u, :], vrows[:].bitcast(F32)[:, u::2], ident[:])
+                    vb = vbank[:].rearrange("p u r -> p (u r)").bitcast(BF16).rearrange("p (u r e) -> p r u e", u=2, e=2)
+                    nc.vector.tensor_copy(out=cols[:].rearrange("p v g (u e) -> p (v g) u e", u=2), in_=vb[:, 0:12])
+                    nc.vector.tensor_scalar(out=b_s[:], in0=cols[:, 0], scalar1=SLOPE, scalar2=None, op0=ALU.mult)
+
+                s_bc = const.tile([P, M], BF16, name="s_bc")
+                pg_bc = const.tile([P, N], BF16, name="pg_bc")
+
+                def spread(dst, lo, src):
+                    sb = bank([P, 512])
+                    nc.tensor.matmul(sb[:], lhsT=ones[:], rhs=rows[:, src : src + 512], start=True, stop=True)
+                    nc.scalar.copy(out=dst[:, lo : lo + 512], in_=sb[:])
+
+                zt, ut, lt, ht = {}, {}, {}, {}
+
+                def z_op(s):
+                    k, t = divmod(s, 4)
+                    zt[s] = bank([P, 512])
+                    mm(zt[s][:], wq[k // 2], P * t, xq[k % 2], 0, 512, True, True)
+
+                def u_op(s):
+                    k, t = divmod(s, 4)
+                    ut[s] = ul_pool.tile([P, 512], F32, name="u", tag="u")
+                    nc.scalar.activation(
+                        out=ut[s][:], in_=zt[s][:], func=ACT.Identity, scale=SLOPE, bias=b_s[:, k // 2, t : t + 1]
+                    )
+
+                def max_op(s):
+                    k, t = divmod(s, 4)
+                    lt[s] = ul_pool.tile([P, 512], F32, name="l", tag="l")
+                    nc.vector.scalar_tensor_tensor(
+                        out=lt[s][:],
+                        in0=zt[s][:],
+                        scalar=cols[:, 0, k // 2, t : t + 1],
+                        in1=ut[s][:],
+                        op0=ALU.add,
+                        op1=ALU.max,
+                    )
+
+                def gain_op(s):
+                    k, t = divmod(s, 4)
+                    if t == 0:
+                        ht[k] = ht_pool.tile([P, 4, 512], BF16, name="ht", tag="ht")
+                    m0 = 512 * (k % 2)
+                    nc.vector.scalar_tensor_tensor(
+                        out=ht[k][:, t, :],
+                        in0=lt[s][:],
+                        scalar=cols[:, 1, k // 2, t : t + 1],
+                        in1=s_bc[:, m0 : m0 + 512],
+                        op0=ALU.mult,
+                        op1=ALU.mult,
+                    )
+
+                ilt, trb, evt = {}, {}, {}
+
+                def il_op(k):
+                    ilt[k] = group_tile()
+                    nc.vector.tensor_copy(out=ilt[k][:], in_=ht[k][:].rearrange("p t m -> p m t"))
+
+                def qa_op(k):
+                    m0 = 512 * (k % 2)
+                    quant(ha[k // 2], m0, m0 + 512, flat(ilt[k]))
+
+                def tr_op(k, i):
+                    trb[(k, i)] = bank([P, 2, 2, P])
+                    for t in range(2):
+                        words = ht[k][:, 2 * i + t, :].bitcast(F32)
+                        for u in range(2):
+                            nc.tensor.transpose(trb[(k, i)][:, t, u, :], words[:, u::2], ident[:])
+
+                def ev_op(k, i):
+                    if i == 0:
+                        evt[k] = group_tile()
+                    gw = flat(evt[k]).bitcast(F32).rearrange("p (t m u) -> p t m u", t=4, u=2)
+                    nc.scalar.copy(out=gw[:, 2 * i : 2 * i + 2], in_=trb[(k, i)][:].rearrange("p t u m -> p t m u"))
+
+                def qc_op(k):
+                    n0 = 512 * (k // 2)
+                    quant(hc[k % 2], n0, n0 + 512, flat(evt[k]))
+
+                qb, qg = {}, {}
+
+                def q_tr(h, r):
+                    qb[(h, r)] = bank([P, 2, 2, P])
+                    words = q_raw[2 * h + r // 2][:, r % 2, :].bitcast(F32)
+                    for c in range(2):
+                        for u in range(2):
+                            nc.tensor.transpose(qb[(h, r)][:, c, u, :], words[:, 256 * c + u : 256 * c + 256 : 2], ident[:])
+
+                def q_ev(h, r):
+                    if r == 0:
+                        qg[h] = raw.tile([P, 2, 512, 4], BF16, name="qg", tag="qg", align_bytes=64)
+                    gw = qg[h][:].rearrange("p c m t -> p (c m t)").bitcast(F32)
+                    gw = gw.rearrange("p (c r m u) -> p c r m u", c=2, r=4, u=2)
+                    nc.scalar.copy(out=gw[:, :, r], in_=qb[(h, r)][:].rearrange("p c u m -> p c m u"))
+
+                def q_quant(h):
+                    for c in range(2):
+                        quant(qq[c], 512 * h, 512 * h + 512, qg[h][:, c].rearrange("p m t -> p (m t)"))
+
+                pwt, pgt, pbk = {}, {}, {}
+
+                def p_widen(i, t0):
+                    g, n = divmod(i, 3)
+                    if t0 == 0:
+                        pwt[i] = pw_pool.tile([P, 4, 512], BF16, name="pw", tag="pw")
+                    for t in (t0, t0 + 1):
+                        src = p_raw[g][:, t, 512 * n : 512 * n + 512].bitcast(FP8)
+                        sc = p_sc[:, g, t : t + 1]
+                        if i in WIDEN_S:
+                            nc.scalar.activation(out=pwt[i][:, t, :], in_=src, func=ACT.Copy, scale=sc)
+                        else:
+                            nc.vector.tensor_scalar(out=pwt[i][:, t, :], in0=src, scalar1=sc, scalar2=None, op0=ALU.mult)
+
+                def p_mm(i, j):
+                    pbk[(i, j)] = bank([P, 2, 512], BF16)
+                    src = pwt[i][:].rearrange("p t m -> p m t")
+                    for e in range(2):
+                        m0 = 256 * j + 128 * e
+                        nc.tensor.matmul(
+                            pbk[(i, j)][:, e, :], lhsT=ident_b[:], rhs=src[:, m0 : m0 + P, :], start=True, stop=True
+                        )
+
+                def p_ev(i, j):
+                    if j == 0:
+                        pgt[i] = group_tile()
+                    nc.scalar.copy(
+                        out=flat(pgt[i])[:, 1024 * j : 1024 * j + 1024],
+                        in_=pbk[(i, j)][:].rearrange("p e c -> p (e c)"),
+                    )
+
+                def p_q(i):
+                    g, n = divmod(i, 3)
+                    quant(pq[g], 512 * n, 512 * n + 512, flat(pgt[i]))
+
+                ctxt, cb = {}, {}
+
+                def c_mm(g, h, t):
+                    cb[(g, h, t)] = bank([P, 512])
+                    for c in range(2):
+                        mm(cb[(g, h, t)][:], hc[c], 512 * g + P * t, qq[c], 512 * h, 512, c == 0, c == 1)
+
+                def c_ev(g, h, t, pool, eng):
+                    if t == 0:
+                        ctxt[(g, h)] = pool.tile([P, 4, 512], F32, name="ctxt%d%d" % (g, h))
+                    src = cb[(g, h, t)]
+                    sc = cols[:, 2, g, t : t + 1]
+                    bi = cols[:, 3, g, t : t + 1]
+                    if eng == "s":
+                        nc.scalar.activation(
+                            out=ctxt[(g, h)][:, t, :], in_=src[:], func=ACT.Identity, scale=sc, bias=bi
+                        )
+                    else:
+                        nc.vector.tensor_scalar(
+                            out=ctxt[(g, h)][:, t, :], in0=src[:], scalar1=sc, scalar2=bi, op0=ALU.mult, op1=ALU.add
+                        )
+
+                x_half(0)
+                w_il(0)
+                columns()
+                x_quant(0)
+                w_quant(0)
+                spread(s_bc, 0, 0)
+                spread(s_bc, 512, 512)
+                nc.vector.tensor_copy(out=ident_b[:], in_=ident[:])
+                z_op(0)
+                z_op(1)
+                u_op(0)
+
+                ops = {
+                    "xh": lambda: x_half(1),
+                    "xq": lambda: x_quant(1),
+                    "wi": w_il,
+                    "wq": w_quant,
+                    "qt": q_tr,
+                    "qe": q_ev,
+                    "qq": q_quant,
+                    "pw": p_widen,
+                    "pm": p_mm,
+                    "pe": p_ev,
+                    "pq": p_q,
+                    "pg": lambda i: spread(pg_bc, 512 * i, M + 512 * i),
+                    "cm": c_mm,
+                    "ce": lambda g, h, t: c_ev(g, h, t, ctxt_pool, "s"),
+                    "il": il_op,
+                    "qa": qa_op,
+                    "tr": tr_op,
+                    "ev": ev_op,
+                    "qc": qc_op,
+                }
+                for s in range(SLOTS):
+                    if s + 2 < 24:
+                        z_op(s + 2)
+                    if s + 1 < 24:
+                        u_op(s + 1)
+                    if s < 24:
+                        max_op(s)
+                    fill = FILL.get(s, ())
+                    for name, args in fill[: len(fill) // 2]:
+                        ops[name](*args)
+                    if 0 < s <= 24:
+                        gain_op(s - 1)
+                    for name, args in fill[len(fill) // 2 :]:
+                        ops[name](*args)
+
+            with tc.tile_pool(name="late1", bufs=1) as late1, tc.tile_pool(name="late", bufs=3) as late:
+                own_v = own_out.rearrange("(r p) n -> r p n", p=P)
+                close_v = close_out.rearrange("(r p) n -> r p n", p=P)
+                ab, sst, rinv, ownt, dt_, tbs = {}, {}, {}, {}, {}, {}
+
+                def a_mm(r, n):
+                    ab[(r, n)] = bank([P, 512])
+                    for g in range(3):
+                        mm(ab[(r, n)][:], ha[g], P * r, pq[g], 512 * n, 512, g == 0, g == 2)
+
+                def sq(r, n):
+                    if n == 0:
+                        sst[r] = small.tile([P, 3], F32, name="ss", tag="ss")
+                    junk = late.tile([P, 512], BF16, name="junk", tag="junk")
+                    nc.scalar.activation(
+                        out=junk[:], in_=ab[(r, n)][:], func=ACT.Square, scale=1.0 / N**0.5, accum_out=sst[r][:, n : n + 1]
+                    )
+
+                def rms(r):
+                    ms = small.tile([P, 2], F32, name="ms", tag="ms")
+                    rinv[r] = small.tile([P, 1], F32, name="rv", tag="rv")
+                    nc.gpsimd.tensor_tensor(out=ms[:, 0:1], in0=sst[r][:, 0:1], in1=sst[r][:, 1:2], op=ALU.add)
+                    nc.gpsimd.tensor_tensor(out=ms[:, 1:2], in0=ms[:, 0:1], in1=sst[r][:, 2:3], op=ALU.add)
+                    nc.gpsimd.tensor_tensor(out=rinv[r][:], in0=ms[:, 1:2], in1=mhalf[:], op=ALU.pow)
+
+                def own_op(r, n):
+                    if n == 0:
+                        ownt[r] = late.tile([P, N], F32, name="own", tag="own")
+                    nc.vector.scalar_tensor_tensor(
+                        out=ownt[r][:, 512 * n : 512 * n + 512],
+                        in0=ab[(r, n)][:],
+                        scalar=rinv[r][:],
+                        in1=pg_bc[:, 512 * n : 512 * n + 512],
+                        op0=ALU.mult,
+                        op1=ALU.mult,
+                    )
+                    if n == 2:
+                        nc.sync.dma_start(out=own_v[r], in_=ownt[r][:])
+
+                def ct(r, g):
+                    tbs[(r, g)] = bank([P, 4, P])
+                    c0 = P * (r % 4)
+                    for t in range(4):
+                        nc.tensor.transpose(tbs[(r, g)][:, t, :], ctxt[(g, r // 4)][:, t, c0 : c0 + P], ident[:])
+
+                def d_op(r, g):
+                    if g == 0:
+                        dt_[r] = late.tile([P, N], F32, name="d", tag="d")
+                    cs = slice(512 * g, 512 * g + 512)
+                    nc.vector.tensor_tensor(
+                        out=dt_[r][:, cs].rearrange("p (m t) -> p m t", t=4),
+                        in0=ownt[r][:, cs].rearrange("p (m t) -> p m t", t=4),
+                        in1=tbs[(r, g)][:].rearrange("p t m -> p m t"),
+                        op=ALU.subtract,
+                    )
+
+                def abs_v(r, lo, hi):
+                    d = dt_[r][:, lo:hi]
+                    nc.vector.scalar_tensor_tensor(out=d, in0=d, scalar=-1.0, in1=d, op0=ALU.mult, op1=ALU.max)
+
+                def abs_s(r, lo, hi):
+                    d = dt_[r][:, lo:hi]
+                    nc.scalar.activation(out=d, in_=d, func=ACT.Abs)
+
+                def exp_s(r, lo, hi):
+                    d = dt_[r][:, lo:hi]
+                    nc.scalar.activation(out=d, in_=d, func=ACT.Exp, scale=-1.0)
+                    nc.sync.dma_start(out=close_v[r][:, lo:hi], in_=d)
+
+                def c2(h):
+                    for t in range(4):
+                        c_mm(2, h, t)
+                        c_ev(2, h, t, late1, "s")
+
+                for n in range(3):
+                    a_mm(0, n)
+                    sq(0, n)
+                rms(0)
+                c2(0)
+                for n in range(3):
+                    own_op(0, n)
+                for n in range(3):
+                    a_mm(1, n)
+                    sq(1, n)
+                rms(1)
+                for r in range(8):
+                    va = VABS[r]
+                    if r + 1 < 8:
+                        for n in range(3):
+                            own_op(r + 1, n)
+                    for g in range(3):
+                        ct(r, g)
+                        d_op(r, g)
+                    if r + 2 < 8:
+                        for n in range(3):
+                            a_mm(r + 2, n)
+                            sq(r + 2, n)
+                        rms(r + 2)
+                    if r == 1:
+                        c2(1)
+                    if r < 7:
+                        if va:
+                            abs_v(r, 0, va)
+                        abs_s(r, va, N)
+                        exp_s(r, 0, N)
+                    else:
+                        abs_v(r, 0, 512)
+                        exp_s(r, 0, 512)
+                        abs_v(r, 512, 1024)
+                        exp_s(r, 512, 1024)
+                        abs_v(r, 1024, N)
+                        exp_s(r, 1024, N)

@@ -15,43 +15,80 @@ FP8X4 = mybir.dt.float8_e4m3fn_x4
 ALU = mybir.AluOpType
 ACT = mybir.ActivationFunctionType
 
-P = 128
 SLOPE = 0.2
+P = 128
+PACK = 4
+PASS = P * PACK
+BANK = 512
+GROUPS = N // PASS
+HALVES = M // PASS
+UNITS = GROUPS * HALVES
+TILES = UNITS * PACK
+ROW_TILES = M // P
+P_PIECES = GROUPS * (N // BANK)
 
-FILL = {
-    0: [('xh', ())],
-    1: [('xq', ()), ('pw', (0, 0)), ('pw', (0, 2))],
-    2: [('pm', (0, 0)), ('pm', (0, 1))],
-    3: [('wi', (1,)), ('tr', (0, 0)), ('pe', (0, 0)), ('pe', (0, 1)), ('pw', (1, 0)), ('pw', (1, 2))],
-    4: [('wq', (1,)), ('ev', (0, 0)), ('pq', (0,)), ('pm', (1, 0)), ('pm', (1, 1))],
-    5: [('il', (0,)), ('tr', (0, 1)), ('qt', (0, 0)), ('pe', (1, 0)), ('pe', (1, 1)), ('pw', (2, 0)), ('pw', (2, 2))],
-    6: [('qa', (0,)), ('ev', (0, 1)), ('qe', (0, 0)), ('qt', (0, 1)), ('pq', (1,)), ('pm', (2, 0)), ('pm', (2, 1))],
-    7: [('qc', (0,)), ('tr', (1, 0)), ('qe', (0, 1)), ('qt', (0, 2)), ('pe', (2, 0)), ('pe', (2, 1))],
-    8: [('ev', (1, 0)), ('qe', (0, 2)), ('qt', (0, 3)), ('pq', (2,)), ('pw', (3, 0)), ('pw', (3, 2))],
-    9: [('il', (1,)), ('tr', (1, 1)), ('qe', (0, 3)), ('pm', (3, 0)), ('pm', (3, 1))],
-    10: [('wi', (2,)), ('qa', (1,)), ('ev', (1, 1)), ('qq', (0,)), ('pe', (3, 0)), ('pe', (3, 1))],
-    11: [('wq', (2,)), ('qc', (1,)), ('tr', (2, 0)), ('qt', (1, 0)), ('pq', (3,)), ('pw', (4, 0)), ('pw', (4, 2))],
-    12: [('ev', (2, 0)), ('qe', (1, 0)), ('qt', (1, 1)), ('pg', (0,)), ('pm', (4, 0)), ('pm', (4, 1))],
-    13: [('il', (2,)), ('tr', (2, 1)), ('qe', (1, 1)), ('qt', (1, 2)), ('pg', (1,)), ('pe', (4, 0)), ('pe', (4, 1)), ('pw', (5, 0)), ('pw', (5, 2))],
-    14: [('qa', (2,)), ('ev', (2, 1)), ('qe', (1, 2)), ('qt', (1, 3)), ('pg', (2,)), ('pq', (4,)), ('pm', (5, 0)), ('pm', (5, 1))],
-    15: [('qc', (2,)), ('tr', (3, 0)), ('qe', (1, 3)), ('pe', (5, 0)), ('pe', (5, 1)), ('pw', (6, 0)), ('pw', (6, 2))],
-    16: [('ev', (3, 0)), ('qq', (1,)), ('pq', (5,)), ('pm', (6, 0)), ('pm', (6, 1))],
-    17: [('il', (3,)), ('tr', (3, 1)), ('pe', (6, 0)), ('pe', (6, 1)), ('pw', (7, 0)), ('pw', (7, 2)), ('cm', (0, 0, 0)), ('ce', (0, 0, 0)), ('cm', (0, 0, 1)), ('ce', (0, 0, 1))],
-    18: [('qa', (3,)), ('ev', (3, 1)), ('pq', (6,)), ('pm', (7, 0)), ('pm', (7, 1)), ('cm', (0, 0, 2)), ('ce', (0, 0, 2)), ('cm', (0, 0, 3)), ('ce', (0, 0, 3))],
-    19: [('qc', (3,)), ('tr', (4, 0)), ('pe', (7, 0)), ('pe', (7, 1)), ('pw', (8, 0)), ('pw', (8, 2)), ('cm', (0, 1, 0)), ('ce', (0, 1, 0)), ('cm', (0, 1, 1)), ('ce', (0, 1, 1))],
-    20: [('ev', (4, 0)), ('pq', (7,)), ('pm', (8, 0)), ('pm', (8, 1)), ('cm', (0, 1, 2)), ('ce', (0, 1, 2)), ('cm', (0, 1, 3)), ('ce', (0, 1, 3))],
-    21: [('il', (4,)), ('tr', (4, 1)), ('pe', (8, 0)), ('pe', (8, 1)), ('cm', (1, 0, 0)), ('ce', (1, 0, 0)), ('cm', (1, 0, 1)), ('ce', (1, 0, 1))],
-    22: [('qa', (4,)), ('ev', (4, 1)), ('pq', (8,)), ('cm', (1, 0, 2)), ('ce', (1, 0, 2)), ('cm', (1, 0, 3)), ('ce', (1, 0, 3))],
-    23: [('qc', (4,)), ('tr', (5, 0)), ('cm', (1, 1, 0)), ('ce', (1, 1, 0)), ('cm', (1, 1, 1)), ('ce', (1, 1, 1))],
-    24: [('ev', (5, 0)), ('cm', (1, 1, 2)), ('ce', (1, 1, 2)), ('cm', (1, 1, 3)), ('ce', (1, 1, 3))],
-    25: [('il', (5,)), ('tr', (5, 1))],
-    26: [('qa', (5,)), ('ev', (5, 1))],
-    27: [('qc', (5,))],
-}
-SLOTS = 28
-GRP_BUFS = 5
-WIDEN_S = {1, 3, 5, 7}
-VABS = [512, 512, 512, 512, 512, 512, 512, 512]
+INTERLEAVE_ON_SCALAR = (0, 2)
+ABS_ON_VECTOR = 768
+
+W_SLOTS = (0, 2)
+W_QUANT_LAG = 5
+Q_SLOTS = (0, 15)
+Q_HALF_STEPS = (5, 0)
+Q_QUANT_LAG = 6
+P_SLOTS = (0, 3, 6, 7, 13, 17, 18, 23, 23)
+P_INTERLEAVE_LAG = 2
+P_QUANT_LAG = 5
+C_SLOTS = (21, 26)
+C_HALF_STEPS = (1, 3)
+C_COPY_LAG = 3
+A_SLOT = 37
+
+
+def woven_work():
+    entries = []
+
+    def put(slot, what, *args):
+        entries.append((slot, len(entries), what, args))
+
+    put(0, "x transposes", 1)
+    put(1, "x quant", 1)
+    for i, slot in enumerate(W_SLOTS):
+        put(slot, "w interleave", i + 1)
+        put(slot + W_QUANT_LAG, "w quant", i + 1)
+    for k in range(UNITS):
+        s = 4 * k
+        put(s + 5, "h transposes", k, 0)
+        put(s + 7, "h copy", k, 0)
+        put(s + 12, "h interleave", k)
+        put(s + 5, "h transposes", k, 1)
+        put(s + 14, "h quant features", k)
+        put(s + 7, "h copy", k, 1)
+        put(s + 11, "h quant samples", k)
+    for m in range(HALVES):
+        for r in range(4):
+            slot = Q_SLOTS[m] + Q_HALF_STEPS[m] * r // 2
+            put(slot, "q transposes", m, r)
+            put(slot + 1, "q copy", m, r)
+        put(slot + 1 + Q_QUANT_LAG, "q quant", m)
+    for i, slot in enumerate(P_SLOTS):
+        put(slot, "p widen", i, 0)
+        put(slot + 1, "p widen", i, 2)
+        put(slot + P_INTERLEAVE_LAG, "p interleave", i)
+        put(slot + P_INTERLEAVE_LAG + P_QUANT_LAG, "p quant", i)
+    for g in range(2):
+        for j in range(8):
+            slot = C_SLOTS[g] + C_HALF_STEPS[g] * j // 2
+            put(slot, "c matmuls", g, j // 4, j % 4)
+            put(slot + C_COPY_LAG, "c copy", g, j // 4, j % 4)
+    for n in range(3):
+        put(A_SLOT, "a matmuls", 0, n)
+        put(A_SLOT, "a squares", 0, n)
+    put(A_SLOT, "a norm", 0)
+
+    work = {}
+    for slot, order, what, args in sorted(entries, key=lambda e: (e[0], e[1])):
+        work.setdefault(slot, []).append((what, args))
+    return work
 
 
 def tile_minibatch_discriminator_features_f6_kernel(
@@ -61,454 +98,475 @@ def tile_minibatch_discriminator_features_f6_kernel(
     with ExitStack() as ctx:
         const = ctx.enter_context(tc.tile_pool(name="const", bufs=1))
         codes = ctx.enter_context(tc.tile_pool(name="codes", bufs=1))
-        grp_pool = ctx.enter_context(tc.tile_pool(name="grp", bufs=GRP_BUFS))
-        pw_pool = ctx.enter_context(tc.tile_pool(name="pw", bufs=2))
-        ht_pool = ctx.enter_context(tc.tile_pool(name="ht", bufs=3))
-        ul_pool = ctx.enter_context(tc.tile_pool(name="ul", bufs=3))
-        small = ctx.enter_context(tc.tile_pool(name="small", bufs=4))
-        ctxt_pool = ctx.enter_context(tc.tile_pool(name="ctxt", bufs=1))
+        grouped_pool = ctx.enter_context(tc.tile_pool(name="grouped", bufs=5))
+        wide_pool = ctx.enter_context(tc.tile_pool(name="wide", bufs=2))
+        h_pool = ctx.enter_context(tc.tile_pool(name="h", bufs=3))
+        leaky_pool = ctx.enter_context(tc.tile_pool(name="leaky", bufs=3))
+        norm_pool = ctx.enter_context(tc.tile_pool(name="norm", bufs=4))
+        context_pool = ctx.enter_context(tc.tile_pool(name="context", bufs=1))
         psum = ctx.enter_context(tc.psum_pool(name="psum", bufs=8))
 
         ident = const.tile([P, P], F32, name="ident")
         make_identity(nc, ident[:])
-        ident_b = const.tile([P, P], BF16, name="ident_b")
 
-        def code_pair(name, width):
-            c = codes.tile([P, width], U32, name=name + "_c", align_bytes=64)
-            s = codes.tile([P, width], U8, name=name + "_s", align_bytes=64)
-            return c, s
+        def bank(shape):
+            return psum.tile(shape, F32, name="bank", tag="bank")
 
-        def quant(pair, lo, hi, src):
-            nc.vector.quantize_mx(out=pair[0][:, lo:hi].bitcast(FP8X4), scales=pair[1][:, lo:hi], in_=src)
+        def grouped_tile():
+            return grouped_pool.tile([P, PASS, PACK], BF16, name="grouped", tag="grouped", align_bytes=64)
 
-        def mm(out, lhs, l0, rhs, r0, n, start, stop):
+        def flat(tile):
+            return tile[:].rearrange("p c t -> p (c t)")
+
+        def operand(name, width):
+            words = codes.tile([P, width], U32, name=name + "_codes", align_bytes=64)
+            scales = codes.tile([P, width], U8, name=name + "_scales", align_bytes=64)
+            return words, scales
+
+        def quantize(op, column, grouped):
+            cols = slice(column, column + PASS)
+            nc.vector.quantize_mx(out=op[0][:, cols].bitcast(FP8X4), scales=op[1][:, cols], in_=grouped)
+
+        def multiply(out, stationary, column, moving, moving_column, start, stop):
+            lhs = slice(column, column + P)
+            rhs = slice(moving_column, moving_column + BANK)
             nc.tensor.matmul_mx(
                 out=out,
-                lhsT=lhs[0][:, l0 : l0 + P].bitcast(FP8X4),
-                lhsT_scale=lhs[1][:, l0 : l0 + P],
-                rhs=rhs[0][:, r0 : r0 + n].bitcast(FP8X4),
-                rhs_scale=rhs[1][:, r0 : r0 + n],
+                lhsT=stationary[0][:, lhs].bitcast(FP8X4),
+                lhsT_scale=stationary[1][:, lhs],
+                rhs=moving[0][:, rhs].bitcast(FP8X4),
+                rhs_scale=moving[1][:, rhs],
                 start=start,
                 stop=stop,
             )
 
-        def bank(shape, dtype=F32):
-            return psum.tile(shape, dtype, name="bank", tag="bank")
+        def transpose_word_pairs(out, words):
+            for u in range(2):
+                nc.tensor.transpose(out[:, u, :], words[:, u::2], ident[:])
 
-        def flat(t):
-            return t[:].rearrange("p m t -> p (m t)")
+        def words_of(grouped, blocks):
+            return flat(grouped).bitcast(F32).rearrange("p (b c u) -> p b c u", b=blocks, u=2)
 
-        def group_tile():
-            return grp_pool.tile([P, 512, 4], BF16, name="grp", tag="grp", align_bytes=64)
+        def interleave(copy, dst, src):
+            copy(
+                out=dst[:].rearrange("p (c i) t -> p c t i", i=4), in_=src[:].rearrange("p t (c i) -> p c t i", i=4)
+            )
 
-        xq = [code_pair("xq%d" % i, 512) for i in range(2)]
-        wq = [code_pair("wq%d" % i, 512) for i in range(3)]
-        ha = [code_pair("ha%d" % i, 1024) for i in range(3)]
-        hc = [code_pair("hc%d" % i, 1536) for i in range(2)]
-        qq = [code_pair("qq%d" % i, 1024) for i in range(2)]
-        pq = [code_pair("pq%d" % i, 1536) for i in range(3)]
+        x_mx = [operand("x%d" % m, PASS) for m in range(HALVES)]
+        w_mx = [operand("w%d" % g, PASS) for g in range(GROUPS)]
+        hf_mx = [operand("hf%d" % g, M) for g in range(GROUPS)]
+        hs_mx = [operand("hs%d" % m, N) for m in range(HALVES)]
+        q_mx = [operand("q%d" % m, M) for m in range(HALVES)]
+        p_mx = [operand("p%d" % g, N) for g in range(GROUPS)]
 
         with tc.manual_schedule():
-            with tc.tile_pool(name="raw", bufs=1) as raw, tc.tile_pool(name="raw4", bufs=6) as raw4:
+            with tc.tile_pool(name="raw", bufs=1) as raw, tc.tile_pool(name="raw_ring", bufs=6) as raw_ring:
                 warm = const.tile([P, 1], F32, name="warm")
-                mhalf = const.tile([P, 1], F32, name="mhalf")
-                vrows = const.tile([P, 512], BF16, name="vrows")
-                rows = raw.tile([P, 2560], BF16, name="rows")
+                minus_half = const.tile([P, 1], F32, name="minus_half")
+                vector_rows = const.tile([P, PASS], BF16, name="vector_rows")
+                sample_row = raw.tile([P, M], BF16, name="sample_row")
                 ones = const.tile([P, P], BF16, name="ones")
                 nc.vector.memset(warm[:], 0.0)
-                nc.vector.memset(vrows[:], 0.0)
-                nc.vector.memset(rows[:], 0.0)
+                nc.vector.memset(vector_rows[:], 0.0)
+                nc.vector.memset(sample_row[:], 0.0)
                 nc.vector.memset(ones[:], 1.0)
-                nc.vector.memset(mhalf[:], -0.5)
+                nc.vector.memset(minus_half[:], -0.5)
 
-                xv = x.rearrange("(h r p) k -> h p r k", p=P, r=4)
-                wv = w.rearrange("(p j) (g c) -> g p j c", j=4, g=3)
-                qv = q.rearrange("(s r p) k -> s p r k", p=P, r=2)
-                pv = p_bytes.rearrange("(g p t) n -> g p t n", p=P, t=4)
-                p_raw = [raw.tile([P, 4, N], U8, name="p_raw%d" % i) for i in range(3)]
-                p_sc = const.tile([P, 3, 4], F32, name="p_sc")
+                p_raw = [raw.tile([P, PACK, N], U8, name="p_raw%d" % g) for g in range(GROUPS)]
+                p_scales = const.tile([P, GROUPS, PACK], F32, name="p_scales")
+                pgain_all = const.tile([P, N], BF16, name="pgain_all")
                 x_raw, w_raw, q_raw = {}, {}, {}
+                x_view = x.rearrange("(m r p) k -> m p r k", p=P, r=4)
+                w_view = w.rearrange("(p j) (g c) -> g p j c", j=PACK, g=GROUPS)
+                q_view = q.rearrange("(s r p) k -> s p r k", p=P, r=2)
+                p_view = p_bytes.rearrange("(g p t) n -> g p t n", p=P, t=PACK)
 
-                def load4(store, i, shape, src):
-                    store[i] = raw4.tile(shape, BF16, name="raw4", tag="raw4")
-                    nc.sync.dma_start(out=store[i][:], in_=src)
+                def load(store, key, view, pieces=1):
+                    shape = [P, 2, M] if store is q_raw else [P, 4, PASS]
+                    store[key] = raw_ring.tile(shape, BF16, name="raw_ring", tag="raw_ring")
+                    step = shape[1] // pieces
+                    for i in range(0, shape[1], step):
+                        nc.sync.dma_start(out=store[key][:, i : i + step], in_=view[key][:, i : i + step])
 
                 def load_p(g):
-                    for i in range(2):
-                        nc.sync.dma_start(out=p_raw[g][:, 2 * i : 2 * i + 2, :], in_=pv[g][:, 2 * i : 2 * i + 2, :])
+                    for t in (0, 2):
+                        nc.sync.dma_start(out=p_raw[g][:, t : t + 2, :], in_=p_view[g][:, t : t + 2, :])
 
-                for v, vec in enumerate((b, fgain, cgain, cbias)):
-                    nc.scalar.dma_start(out=vrows[3 * v : 3 * v + 3, :], in_=vec.rearrange("(g c) -> g c", g=3))
-                nc.scalar.dma_start(out=rows[0:1, 0:M], in_=sweight.rearrange("(o m) -> o m", o=1))
-                nc.scalar.dma_start(out=rows[0:1, M : M + N], in_=pgain.rearrange("(o m) -> o m", o=1))
-                load4(x_raw, 0, [P, 4, K], xv[0])
-                load4(w_raw, 0, [P, 4, 512], wv[0])
-                load4(x_raw, 1, [P, 4, K], xv[1])
-                nc.sync.dma_start(out=p_sc[:], in_=p_scale.rearrange("(g p t) o -> p g (t o)", p=P, t=4))
+                for i, vector in enumerate((b, fgain, cgain, cbias)):
+                    nc.scalar.dma_start(
+                        out=vector_rows[GROUPS * i : GROUPS * i + GROUPS, :],
+                        in_=vector.rearrange("(g c) -> g c", g=GROUPS),
+                    )
+                nc.scalar.dma_start(out=sample_row[0:1, :], in_=sweight.rearrange("(o m) -> o m", o=1))
+                load(w_raw, 0, w_view)
+                load(x_raw, 0, x_view, pieces=2)
+                load(x_raw, 1, x_view)
+                nc.sync.dma_start(out=p_scales[:], in_=p_scale.rearrange("(g p t) o -> p g (t o)", p=P, t=PACK))
                 load_p(0)
-                load4(w_raw, 1, [P, 4, 512], wv[1])
-                load4(q_raw, 0, [P, 2, M], qv[0])
-                load4(q_raw, 1, [P, 2, M], qv[1])
-                load4(w_raw, 2, [P, 4, 512], wv[2])
+                load(w_raw, 1, w_view)
+                load(q_raw, 0, q_view)
+                load(q_raw, 1, q_view)
+                load(w_raw, 2, w_view)
                 load_p(1)
-                load4(q_raw, 2, [P, 2, M], qv[2])
-                load4(q_raw, 3, [P, 2, M], qv[3])
+                load(q_raw, 2, q_view)
+                load(q_raw, 3, q_view)
                 load_p(2)
+                nc.sync.dma_start(out=pgain_all[:], in_=pgain.partition_broadcast(P))
 
                 nc.scalar.activation(out=warm[:], in_=warm[:], func=ACT.Exp)
 
-                gx = {}
+                x_grouped, w_grouped = {}, {}
 
-                def x_half(h):
-                    gx[h] = group_tile()
-                    gw = flat(gx[h]).bitcast(F32).rearrange("p (r m u) -> p r m u", r=4, u=2)
-                    for i in range(2):
-                        tb = bank([P, 2, 2, P])
+                def x_transposes(m):
+                    x_grouped[m] = grouped_tile()
+                    words = words_of(x_grouped[m], 4)
+                    for i, copy in enumerate((nc.vector.tensor_copy, nc.scalar.copy)):
+                        turned = bank([P, 2, 2, P])
                         for r in range(2):
-                            words = x_raw[h][:, 2 * i + r, :].bitcast(F32)
-                            for u in range(2):
-                                nc.tensor.transpose(tb[:, r, u, :], words[:, u::2], ident[:])
-                        src = tb[:].rearrange("p r u m -> p r m u")
-                        if i == 0:
-                            nc.vector.tensor_copy(out=gw[:, 2 * i : 2 * i + 2], in_=src)
-                        else:
-                            nc.scalar.copy(out=gw[:, 2 * i : 2 * i + 2], in_=src)
+                            transpose_word_pairs(turned[:, r], x_raw[m][:, 2 * i + r, :].bitcast(F32))
+                        copy(out=words[:, 2 * i : 2 * i + 2], in_=turned[:].rearrange("p r u c -> p r c u"))
 
-                def x_quant(h):
-                    quant(xq[h], 0, 512, flat(gx[h]))
+                def x_quant(m):
+                    quantize(x_mx[m], 0, flat(x_grouped[m]))
 
-                gw_ = {}
-
-                def w_il(g):
-                    gw_[g] = group_tile()
-                    nc.vector.tensor_copy(
-                        out=gw_[g][:].rearrange("p (t m) j -> p t m j", t=4),
-                        in_=w_raw[g][:].rearrange("p j (m t) -> p t m j", t=4),
-                    )
+                def w_interleave(g):
+                    w_grouped[g] = grouped_tile()
+                    dst = w_grouped[g][:].rearrange("p (t j) k -> p j k t", t=PACK)
+                    src = w_raw[g][:].rearrange("p k (j t) -> p j k t", t=PACK)
+                    if g == 0:
+                        nc.vector.tensor_copy(out=dst[:, :, :, 0:2], in_=src[:, :, :, 0:2])
+                        nc.scalar.copy(out=dst[:, :, :, 2:4], in_=src[:, :, :, 2:4])
+                    else:
+                        nc.vector.tensor_copy(out=dst, in_=src)
 
                 def w_quant(g):
-                    quant(wq[g], 0, 512, flat(gw_[g]))
+                    quantize(w_mx[g], 0, flat(w_grouped[g]))
 
-                cols = const.tile([P, 4, 3, 4], F32, name="cols")
-                b_s = const.tile([P, 3, 4], F32, name="b_s")
+                columns = const.tile([P, 4, GROUPS, PACK], F32, name="columns")
+                b_slope = const.tile([P, GROUPS, PACK], F32, name="b_slope")
+                b_col, fgain_col, cgain_col, cbias_col = (columns[:, i] for i in range(4))
+                sweight_all = const.tile([P, M], BF16, name="sweight_all")
 
-                def columns():
-                    vbank = bank([P, 2, P])
-                    for u in range(2):
-                        nc.tensor.transpose(vbank[:, u, :], vrows[:].bitcast(F32)[:, u::2], ident[:])
-                    vb = vbank[:].rearrange("p u r -> p (u r)").bitcast(BF16).rearrange("p (u r e) -> p r u e", u=2, e=2)
-                    nc.vector.tensor_copy(out=cols[:].rearrange("p v g (u e) -> p (v g) u e", u=2), in_=vb[:, 0:12])
-                    nc.vector.tensor_scalar(out=b_s[:], in0=cols[:, 0], scalar1=SLOPE, scalar2=None, op0=ALU.mult)
+                def feature_columns():
+                    turned = bank([P, 2, P])
+                    transpose_word_pairs(turned, vector_rows[:].bitcast(F32))
+                    values = turned[:].rearrange("p u r -> p (u r)").bitcast(BF16)
+                    values = values.rearrange("p (u r e) -> p r u e", u=2, e=2)
+                    nc.vector.tensor_copy(
+                        out=columns[:].rearrange("p i g (u e) -> p (i g) u e", u=2), in_=values[:, 0 : 4 * GROUPS]
+                    )
+                    nc.vector.tensor_scalar(out=b_slope[:], in0=b_col, scalar1=SLOPE, scalar2=None, op0=ALU.mult)
 
-                s_bc = const.tile([P, M], BF16, name="s_bc")
-                pg_bc = const.tile([P, N], BF16, name="pg_bc")
+                def spread_sweight():
+                    for m0 in range(0, M, BANK):
+                        spread = bank([P, BANK])
+                        nc.tensor.matmul(
+                            spread[:], lhsT=ones[:], rhs=sample_row[:, m0 : m0 + BANK], start=True, stop=True
+                        )
+                        nc.scalar.copy(out=sweight_all[:, m0 : m0 + BANK], in_=spread[:])
 
-                def spread(dst, lo, src):
-                    sb = bank([P, 512])
-                    nc.tensor.matmul(sb[:], lhsT=ones[:], rhs=rows[:, src : src + 512], start=True, stop=True)
-                    nc.scalar.copy(out=dst[:, lo : lo + 512], in_=sb[:])
+                z_bank, lower, leaky, h_tile = {}, {}, {}, {}
 
-                zt, ut, lt, ht = {}, {}, {}, {}
+                def z_matmul(s):
+                    k, t = divmod(s, PACK)
+                    z_bank[s] = bank([P, BANK])
+                    multiply(z_bank[s][:], w_mx[k // 2], P * t, x_mx[k % 2], 0, True, True)
 
-                def z_op(s):
-                    k, t = divmod(s, 4)
-                    zt[s] = bank([P, 512])
-                    mm(zt[s][:], wq[k // 2], P * t, xq[k % 2], 0, 512, True, True)
-
-                def u_op(s):
-                    k, t = divmod(s, 4)
-                    ut[s] = ul_pool.tile([P, 512], F32, name="u", tag="u")
+                def leaky_lower(s):
+                    k, t = divmod(s, PACK)
+                    lower[s] = leaky_pool.tile([P, BANK], F32, name="lower", tag="lower")
                     nc.scalar.activation(
-                        out=ut[s][:], in_=zt[s][:], func=ACT.Identity, scale=SLOPE, bias=b_s[:, k // 2, t : t + 1]
+                        out=lower[s][:],
+                        in_=z_bank[s][:],
+                        func=ACT.Identity,
+                        scale=SLOPE,
+                        bias=b_slope[:, k // 2, t : t + 1],
                     )
 
-                def max_op(s):
-                    k, t = divmod(s, 4)
-                    lt[s] = ul_pool.tile([P, 512], F32, name="l", tag="l")
+                def leaky_max(s):
+                    k, t = divmod(s, PACK)
+                    leaky[s] = leaky_pool.tile([P, BANK], F32, name="leaky", tag="leaky")
                     nc.vector.scalar_tensor_tensor(
-                        out=lt[s][:],
-                        in0=zt[s][:],
-                        scalar=cols[:, 0, k // 2, t : t + 1],
-                        in1=ut[s][:],
+                        out=leaky[s][:],
+                        in0=z_bank[s][:],
+                        scalar=b_col[:, k // 2, t : t + 1],
+                        in1=lower[s][:],
                         op0=ALU.add,
                         op1=ALU.max,
                     )
 
-                def gain_op(s):
-                    k, t = divmod(s, 4)
+                def gains(s):
+                    k, t = divmod(s, PACK)
                     if t == 0:
-                        ht[k] = ht_pool.tile([P, 4, 512], BF16, name="ht", tag="ht")
-                    m0 = 512 * (k % 2)
+                        h_tile[k] = h_pool.tile([P, PACK, BANK], BF16, name="h", tag="h")
+                    m0 = BANK * (k % 2)
                     nc.vector.scalar_tensor_tensor(
-                        out=ht[k][:, t, :],
-                        in0=lt[s][:],
-                        scalar=cols[:, 1, k // 2, t : t + 1],
-                        in1=s_bc[:, m0 : m0 + 512],
+                        out=h_tile[k][:, t, :],
+                        in0=leaky[s][:],
+                        scalar=fgain_col[:, k // 2, t : t + 1],
+                        in1=sweight_all[:, m0 : m0 + BANK],
                         op0=ALU.mult,
                         op1=ALU.mult,
                     )
 
-                ilt, trb, evt = {}, {}, {}
+                hf_grouped = {}
 
-                def il_op(k):
-                    ilt[k] = group_tile()
-                    nc.vector.tensor_copy(out=ilt[k][:], in_=ht[k][:].rearrange("p t m -> p m t"))
+                def h_interleave(k):
+                    hf_grouped[k] = grouped_tile()
+                    copy = nc.scalar.copy if k in INTERLEAVE_ON_SCALAR else nc.vector.tensor_copy
+                    interleave(copy, hf_grouped[k], h_tile[k])
 
-                def qa_op(k):
-                    m0 = 512 * (k % 2)
-                    quant(ha[k // 2], m0, m0 + 512, flat(ilt[k]))
+                def h_quant_features(k):
+                    quantize(hf_mx[k // 2], PASS * (k % 2), flat(hf_grouped[k]))
 
-                def tr_op(k, i):
-                    trb[(k, i)] = bank([P, 2, 2, P])
+                h_turned, hs_grouped = {}, {}
+
+                def h_transposes(k, i):
+                    h_turned[(k, i)] = bank([P, 2, 2, P])
                     for t in range(2):
-                        words = ht[k][:, 2 * i + t, :].bitcast(F32)
-                        for u in range(2):
-                            nc.tensor.transpose(trb[(k, i)][:, t, u, :], words[:, u::2], ident[:])
+                        transpose_word_pairs(h_turned[(k, i)][:, t], h_tile[k][:, 2 * i + t, :].bitcast(F32))
 
-                def ev_op(k, i):
+                def h_copy(k, i):
                     if i == 0:
-                        evt[k] = group_tile()
-                    gw = flat(evt[k]).bitcast(F32).rearrange("p (t m u) -> p t m u", t=4, u=2)
-                    nc.scalar.copy(out=gw[:, 2 * i : 2 * i + 2], in_=trb[(k, i)][:].rearrange("p t u m -> p t m u"))
-
-                def qc_op(k):
-                    n0 = 512 * (k // 2)
-                    quant(hc[k % 2], n0, n0 + 512, flat(evt[k]))
-
-                qb, qg = {}, {}
-
-                def q_tr(h, r):
-                    qb[(h, r)] = bank([P, 2, 2, P])
-                    words = q_raw[2 * h + r // 2][:, r % 2, :].bitcast(F32)
-                    for c in range(2):
-                        for u in range(2):
-                            nc.tensor.transpose(qb[(h, r)][:, c, u, :], words[:, 256 * c + u : 256 * c + 256 : 2], ident[:])
-
-                def q_ev(h, r):
-                    if r == 0:
-                        qg[h] = raw.tile([P, 2, 512, 4], BF16, name="qg", tag="qg", align_bytes=64)
-                    gw = qg[h][:].rearrange("p c m t -> p (c m t)").bitcast(F32)
-                    gw = gw.rearrange("p (c r m u) -> p c r m u", c=2, r=4, u=2)
-                    nc.scalar.copy(out=gw[:, :, r], in_=qb[(h, r)][:].rearrange("p c u m -> p c m u"))
-
-                def q_quant(h):
-                    for c in range(2):
-                        quant(qq[c], 512 * h, 512 * h + 512, qg[h][:, c].rearrange("p m t -> p (m t)"))
-
-                pwt, pgt, pbk = {}, {}, {}
-
-                def p_widen(i, t0):
-                    g, n = divmod(i, 3)
-                    if t0 == 0:
-                        pwt[i] = pw_pool.tile([P, 4, 512], BF16, name="pw", tag="pw")
-                    for t in (t0, t0 + 1):
-                        src = p_raw[g][:, t, 512 * n : 512 * n + 512].bitcast(FP8)
-                        sc = p_sc[:, g, t : t + 1]
-                        if i in WIDEN_S:
-                            nc.scalar.activation(out=pwt[i][:, t, :], in_=src, func=ACT.Copy, scale=sc)
-                        else:
-                            nc.vector.tensor_scalar(out=pwt[i][:, t, :], in0=src, scalar1=sc, scalar2=None, op0=ALU.mult)
-
-                def p_mm(i, j):
-                    pbk[(i, j)] = bank([P, 2, 512], BF16)
-                    src = pwt[i][:].rearrange("p t m -> p m t")
-                    for e in range(2):
-                        m0 = 256 * j + 128 * e
-                        nc.tensor.matmul(
-                            pbk[(i, j)][:, e, :], lhsT=ident_b[:], rhs=src[:, m0 : m0 + P, :], start=True, stop=True
-                        )
-
-                def p_ev(i, j):
-                    if j == 0:
-                        pgt[i] = group_tile()
+                        hs_grouped[k] = grouped_tile()
                     nc.scalar.copy(
-                        out=flat(pgt[i])[:, 1024 * j : 1024 * j + 1024],
-                        in_=pbk[(i, j)][:].rearrange("p e c -> p (e c)"),
+                        out=words_of(hs_grouped[k], 4)[:, 2 * i : 2 * i + 2],
+                        in_=h_turned[(k, i)][:].rearrange("p t u c -> p t c u"),
                     )
 
-                def p_q(i):
+                def h_quant_samples(k):
+                    quantize(hs_mx[k % 2], PASS * (k // 2), flat(hs_grouped[k]))
+
+                q_turned, q_grouped = {}, {}
+
+                def q_transposes(m, r):
+                    q_turned[(m, r)] = bank([P, 2, 2, P])
+                    words = q_raw[2 * m + r // 2][:, r % 2, :].bitcast(F32)
+                    for c in range(HALVES):
+                        transpose_word_pairs(q_turned[(m, r)][:, c], words[:, 256 * c : 256 * c + 256])
+
+                def q_copy(m, r):
+                    if r == 0:
+                        q_grouped[m] = raw.tile(
+                            [P, HALVES, PASS, PACK], BF16, name="q_grouped", tag="q_grouped", align_bytes=64
+                        )
+                    words = q_grouped[m][:].rearrange("p c s t -> p (c s t)").bitcast(F32)
+                    words = words.rearrange("p (c r s u) -> p c r s u", c=HALVES, r=4, u=2)
+                    nc.scalar.copy(out=words[:, :, r], in_=q_turned[(m, r)][:].rearrange("p c u s -> p c s u"))
+
+                def q_quant(m):
+                    for c in range(HALVES):
+                        quantize(q_mx[c], PASS * m, q_grouped[m][:, c].rearrange("p s t -> p (s t)"))
+
+                p_wide, p_grouped = {}, {}
+
+                def p_widen(i, first):
                     g, n = divmod(i, 3)
-                    quant(pq[g], 512 * n, 512 * n + 512, flat(pgt[i]))
-
-                ctxt, cb = {}, {}
-
-                def c_mm(g, h, t):
-                    cb[(g, h, t)] = bank([P, 512])
-                    for c in range(2):
-                        mm(cb[(g, h, t)][:], hc[c], 512 * g + P * t, qq[c], 512 * h, 512, c == 0, c == 1)
-
-                def c_ev(g, h, t, pool, eng):
-                    if t == 0:
-                        ctxt[(g, h)] = pool.tile([P, 4, 512], F32, name="ctxt%d%d" % (g, h))
-                    src = cb[(g, h, t)]
-                    sc = cols[:, 2, g, t : t + 1]
-                    bi = cols[:, 3, g, t : t + 1]
-                    if eng == "s":
+                    if first == 0:
+                        p_wide[i] = wide_pool.tile([P, PACK, BANK], BF16, name="wide", tag="wide")
+                    for t in (first, first + 1):
                         nc.scalar.activation(
-                            out=ctxt[(g, h)][:, t, :], in_=src[:], func=ACT.Identity, scale=sc, bias=bi
-                        )
-                    else:
-                        nc.vector.tensor_scalar(
-                            out=ctxt[(g, h)][:, t, :], in0=src[:], scalar1=sc, scalar2=bi, op0=ALU.mult, op1=ALU.add
+                            out=p_wide[i][:, t, :],
+                            in_=p_raw[g][:, t, BANK * n : BANK * n + BANK].bitcast(FP8),
+                            func=ACT.Copy,
+                            scale=p_scales[:, g, t : t + 1],
                         )
 
-                x_half(0)
-                w_il(0)
-                columns()
+                def p_interleave(i):
+                    p_grouped[i] = grouped_tile()
+                    interleave(nc.vector.tensor_copy, p_grouped[i], p_wide[i])
+
+                def p_quant(i):
+                    g, n = divmod(i, 3)
+                    quantize(p_mx[g], PASS * n, flat(p_grouped[i]))
+
+                c_bank, context = {}, {}
+
+                def c_matmuls(g, m, t):
+                    c_bank[(g, m, t)] = bank([P, BANK])
+                    for c in range(HALVES):
+                        multiply(
+                            c_bank[(g, m, t)][:], hs_mx[c], PASS * g + P * t, q_mx[c], BANK * m, c == 0, c == HALVES - 1
+                        )
+
+                def c_copy(g, m, t, pool=context_pool):
+                    if t == 0:
+                        context[(g, m)] = pool.tile([P, PACK, BANK], F32, name="context%d%d" % (g, m))
+                    nc.scalar.activation(
+                        out=context[(g, m)][:, t, :],
+                        in_=c_bank[(g, m, t)][:],
+                        func=ACT.Identity,
+                        scale=cgain_col[:, g, t : t + 1],
+                        bias=cbias_col[:, g, t : t + 1],
+                    )
+
+                a_bank, squares, inverse = {}, {}, {}
+
+                def a_matmuls(r, n):
+                    a_bank[(r, n)] = bank([P, BANK])
+                    for g in range(GROUPS):
+                        multiply(a_bank[(r, n)][:], hf_mx[g], P * r, p_mx[g], BANK * n, g == 0, g == GROUPS - 1)
+
+                def a_squares(r, n):
+                    if n == 0:
+                        squares[r] = norm_pool.tile([P, 3], F32, name="squares", tag="squares")
+                    unused = norm_pool.tile([P, BANK], BF16, name="unused", tag="unused")
+                    nc.scalar.activation(
+                        out=unused[:],
+                        in_=a_bank[(r, n)][:],
+                        func=ACT.Square,
+                        scale=1.0 / N**0.5,
+                        accum_out=squares[r][:, n : n + 1],
+                    )
+
+                def a_norm(r):
+                    mean = norm_pool.tile([P, 1], F32, name="mean", tag="mean")
+                    inverse[r] = norm_pool.tile([P, 1], F32, name="inverse", tag="inverse")
+                    parts = squares[r]
+                    nc.gpsimd.tensor_scalar(
+                        out=mean[:], in0=parts[:, 0:1], scalar1=parts[:, 1:2], scalar2=parts[:, 2:3], op0=ALU.add, op1=ALU.add
+                    )
+                    nc.gpsimd.tensor_tensor(out=inverse[r][:], in0=mean[:], in1=minus_half[:], op=ALU.pow)
+
+                w_interleave(0)
+                x_transposes(0)
+                feature_columns()
                 x_quant(0)
                 w_quant(0)
-                spread(s_bc, 0, 0)
-                spread(s_bc, 512, 512)
-                nc.vector.tensor_copy(out=ident_b[:], in_=ident[:])
-                z_op(0)
-                z_op(1)
-                u_op(0)
+                spread_sweight()
+                z_matmul(0)
+                z_matmul(1)
+                leaky_lower(0)
 
-                ops = {
-                    "xh": lambda: x_half(1),
-                    "xq": lambda: x_quant(1),
-                    "wi": w_il,
-                    "wq": w_quant,
-                    "qt": q_tr,
-                    "qe": q_ev,
-                    "qq": q_quant,
-                    "pw": p_widen,
-                    "pm": p_mm,
-                    "pe": p_ev,
-                    "pq": p_q,
-                    "pg": lambda i: spread(pg_bc, 512 * i, M + 512 * i),
-                    "cm": c_mm,
-                    "ce": lambda g, h, t: c_ev(g, h, t, ctxt_pool, "s"),
-                    "il": il_op,
-                    "qa": qa_op,
-                    "tr": tr_op,
-                    "ev": ev_op,
-                    "qc": qc_op,
+                does = {
+                    "x transposes": x_transposes,
+                    "x quant": x_quant,
+                    "w interleave": w_interleave,
+                    "w quant": w_quant,
+                    "h transposes": h_transposes,
+                    "h copy": h_copy,
+                    "h quant samples": h_quant_samples,
+                    "h interleave": h_interleave,
+                    "h quant features": h_quant_features,
+                    "q transposes": q_transposes,
+                    "q copy": q_copy,
+                    "q quant": q_quant,
+                    "p widen": p_widen,
+                    "p interleave": p_interleave,
+                    "p quant": p_quant,
+                    "c matmuls": c_matmuls,
+                    "c copy": c_copy,
+                    "a matmuls": a_matmuls,
+                    "a squares": a_squares,
+                    "a norm": a_norm,
                 }
-                for s in range(SLOTS):
-                    if s + 2 < 24:
-                        z_op(s + 2)
-                    if s + 1 < 24:
-                        u_op(s + 1)
-                    if s < 24:
-                        max_op(s)
-                    fill = FILL.get(s, ())
-                    for name, args in fill[: len(fill) // 2]:
-                        ops[name](*args)
-                    if 0 < s <= 24:
-                        gain_op(s - 1)
-                    for name, args in fill[len(fill) // 2 :]:
-                        ops[name](*args)
+                work = woven_work()
+                for s in range(max(work) + 1):
+                    if s + 2 < TILES:
+                        z_matmul(s + 2)
+                    if s + 1 < TILES:
+                        leaky_lower(s + 1)
+                    if s < TILES:
+                        leaky_max(s)
+                    here = work.get(s, [])
+                    for what, args in here[: len(here) // 2]:
+                        does[what](*args)
+                    if 0 < s <= TILES:
+                        gains(s - 1)
+                    for what, args in here[len(here) // 2 :]:
+                        does[what](*args)
 
-            with tc.tile_pool(name="late1", bufs=1) as late1, tc.tile_pool(name="late", bufs=3) as late:
-                own_v = own_out.rearrange("(r p) n -> r p n", p=P)
-                close_v = close_out.rearrange("(r p) n -> r p n", p=P)
-                ab, sst, rinv, ownt, dt_, tbs = {}, {}, {}, {}, {}, {}
+            with (
+                tc.tile_pool(name="context_last", bufs=1) as context_last,
+                tc.tile_pool(name="own", bufs=4) as own_pool,
+                tc.tile_pool(name="difference", bufs=3) as difference_pool,
+            ):
+                own_view = own_out.rearrange("(r p) n -> r p n", p=P)
+                close_view = close_out.rearrange("(r p) n -> r p n", p=P)
+                own, difference, context_bank = {}, {}, {}
 
-                def a_mm(r, n):
-                    ab[(r, n)] = bank([P, 512])
-                    for g in range(3):
-                        mm(ab[(r, n)][:], ha[g], P * r, pq[g], 512 * n, 512, g == 0, g == 2)
-
-                def sq(r, n):
+                def own_columns(r, n):
                     if n == 0:
-                        sst[r] = small.tile([P, 3], F32, name="ss", tag="ss")
-                    junk = late.tile([P, 512], BF16, name="junk", tag="junk")
-                    nc.scalar.activation(
-                        out=junk[:], in_=ab[(r, n)][:], func=ACT.Square, scale=1.0 / N**0.5, accum_out=sst[r][:, n : n + 1]
-                    )
-
-                def rms(r):
-                    ms = small.tile([P, 2], F32, name="ms", tag="ms")
-                    rinv[r] = small.tile([P, 1], F32, name="rv", tag="rv")
-                    nc.gpsimd.tensor_tensor(out=ms[:, 0:1], in0=sst[r][:, 0:1], in1=sst[r][:, 1:2], op=ALU.add)
-                    nc.gpsimd.tensor_tensor(out=ms[:, 1:2], in0=ms[:, 0:1], in1=sst[r][:, 2:3], op=ALU.add)
-                    nc.gpsimd.tensor_tensor(out=rinv[r][:], in0=ms[:, 1:2], in1=mhalf[:], op=ALU.pow)
-
-                def own_op(r, n):
-                    if n == 0:
-                        ownt[r] = late.tile([P, N], F32, name="own", tag="own")
+                        own[r] = own_pool.tile([P, N], F32, name="own", tag="own")
+                    cols = slice(BANK * n, BANK * n + BANK)
                     nc.vector.scalar_tensor_tensor(
-                        out=ownt[r][:, 512 * n : 512 * n + 512],
-                        in0=ab[(r, n)][:],
-                        scalar=rinv[r][:],
-                        in1=pg_bc[:, 512 * n : 512 * n + 512],
+                        out=own[r][:, cols],
+                        in0=a_bank[(r, n)][:],
+                        scalar=inverse[r][:],
+                        in1=pgain_all[:, cols],
                         op0=ALU.mult,
                         op1=ALU.mult,
                     )
-                    if n == 2:
-                        nc.sync.dma_start(out=own_v[r], in_=ownt[r][:])
 
-                def ct(r, g):
-                    tbs[(r, g)] = bank([P, 4, P])
-                    c0 = P * (r % 4)
-                    for t in range(4):
-                        nc.tensor.transpose(tbs[(r, g)][:, t, :], ctxt[(g, r // 4)][:, t, c0 : c0 + P], ident[:])
+                def own_rows(r):
+                    for n in range(3):
+                        own_columns(r, n)
+                    nc.sync.dma_start(out=own_view[r], in_=own[r][:])
 
-                def d_op(r, g):
+                def a_rows(r):
+                    for n in range(3):
+                        a_matmuls(r, n)
+                        a_squares(r, n)
+                    a_norm(r)
+
+                def context_transposes(r, g):
+                    context_bank[(r, g)] = bank([P, PACK, P])
+                    m, c0 = r // 4, P * (r % 4)
+                    for t in range(PACK):
+                        nc.tensor.transpose(
+                            context_bank[(r, g)][:, t, :], context[(g, m)][:, t, c0 : c0 + P], ident[:]
+                        )
+
+                def subtract_context(r, g):
                     if g == 0:
-                        dt_[r] = late.tile([P, N], F32, name="d", tag="d")
-                    cs = slice(512 * g, 512 * g + 512)
+                        difference[r] = difference_pool.tile([P, N], F32, name="difference", tag="difference")
+                    cols = slice(PASS * g, PASS * g + PASS)
                     nc.vector.tensor_tensor(
-                        out=dt_[r][:, cs].rearrange("p (m t) -> p m t", t=4),
-                        in0=ownt[r][:, cs].rearrange("p (m t) -> p m t", t=4),
-                        in1=tbs[(r, g)][:].rearrange("p t m -> p m t"),
+                        out=difference[r][:, cols].rearrange("p (j t) -> p j t", t=PACK),
+                        in0=own[r][:, cols].rearrange("p (j t) -> p j t", t=PACK),
+                        in1=context_bank[(r, g)][:].rearrange("p t j -> p j t"),
                         op=ALU.subtract,
                     )
 
-                def abs_v(r, lo, hi):
-                    d = dt_[r][:, lo:hi]
+                def absolute_on_vector(r, lo, hi):
+                    d = difference[r][:, lo:hi]
                     nc.vector.scalar_tensor_tensor(out=d, in0=d, scalar=-1.0, in1=d, op0=ALU.mult, op1=ALU.max)
 
-                def abs_s(r, lo, hi):
-                    d = dt_[r][:, lo:hi]
+                def absolute_on_scalar(r, lo, hi):
+                    d = difference[r][:, lo:hi]
                     nc.scalar.activation(out=d, in_=d, func=ACT.Abs)
 
-                def exp_s(r, lo, hi):
-                    d = dt_[r][:, lo:hi]
+                def closeness(r, lo, hi):
+                    d = difference[r][:, lo:hi]
                     nc.scalar.activation(out=d, in_=d, func=ACT.Exp, scale=-1.0)
-                    nc.sync.dma_start(out=close_v[r][:, lo:hi], in_=d)
+                    nc.sync.dma_start(out=close_view[r][:, lo:hi], in_=d)
 
-                def c2(h):
-                    for t in range(4):
-                        c_mm(2, h, t)
-                        c_ev(2, h, t, late1, "s")
+                def last_context(m, t):
+                    c_matmuls(GROUPS - 1, m, t)
+                    c_copy(GROUPS - 1, m, t, context_last)
 
-                for n in range(3):
-                    a_mm(0, n)
-                    sq(0, n)
-                rms(0)
-                c2(0)
-                for n in range(3):
-                    own_op(0, n)
-                for n in range(3):
-                    a_mm(1, n)
-                    sq(1, n)
-                rms(1)
-                for r in range(8):
-                    va = VABS[r]
-                    if r + 1 < 8:
-                        for n in range(3):
-                            own_op(r + 1, n)
-                    for g in range(3):
-                        ct(r, g)
-                        d_op(r, g)
-                    if r + 2 < 8:
-                        for n in range(3):
-                            a_mm(r + 2, n)
-                            sq(r + 2, n)
-                        rms(r + 2)
-                    if r == 1:
-                        c2(1)
-                    if r < 7:
-                        if va:
-                            abs_v(r, 0, va)
-                        abs_s(r, va, N)
-                        exp_s(r, 0, N)
+                for t in range(PACK):
+                    last_context(0, t)
+                a_rows(1)
+                own_rows(0)
+                for r in range(ROW_TILES):
+                    for g in range(GROUPS):
+                        context_transposes(r, g)
+                    for g in range(GROUPS):
+                        subtract_context(r, g)
+                    if r < 2:
+                        last_context(1, r)
+                    elif r == 2:
+                        last_context(1, 2)
+                        last_context(1, 3)
+                    if r + 1 < ROW_TILES:
+                        own_rows(r + 1)
+                        absolute_on_scalar(r, ABS_ON_VECTOR, N)
+                        if r + 2 < ROW_TILES:
+                            a_rows(r + 2)
+                        absolute_on_vector(r, 0, ABS_ON_VECTOR)
+                        closeness(r, 0, N)
                     else:
-                        abs_v(r, 0, 512)
-                        exp_s(r, 0, 512)
-                        abs_v(r, 512, 1024)
-                        exp_s(r, 512, 1024)
-                        abs_v(r, 1024, N)
-                        exp_s(r, 1024, N)
+                        for n in range(3):
+                            absolute_on_vector(r, BANK * n, BANK * n + BANK)
+                            closeness(r, BANK * n, BANK * n + BANK)

@@ -163,12 +163,12 @@ def tile_minibatch_discriminator_features_f6_kernel(
             with tc.tile_pool(name="raw", bufs=1) as raw, tc.tile_pool(name="raw_ring", bufs=6) as raw_ring:
                 warm = const.tile([P, 1], F32, name="warm")
                 minus_half = const.tile([P, 1], F32, name="minus_half")
-                vector_rows = const.tile([P, PASS], BF16, name="vector_rows")
+                vector_rows = raw.tile([P, N], BF16, name="vector_rows")
                 sample_row = raw.tile([P, M], BF16, name="sample_row")
                 ones = const.tile([P, P], BF16, name="ones")
-                nc.vector.memset(warm[:], 0.0)
                 nc.vector.memset(vector_rows[:], 0.0)
                 nc.vector.memset(sample_row[:], 0.0)
+                nc.vector.memset(warm[:], 0.0)
                 nc.vector.memset(ones[:], 1.0)
                 nc.vector.memset(minus_half[:], -0.5)
 
@@ -193,10 +193,7 @@ def tile_minibatch_discriminator_features_f6_kernel(
                         nc.sync.dma_start(out=p_raw[g][:, t : t + 2, :], in_=p_view[g][:, t : t + 2, :])
 
                 for i, vector in enumerate((b, fgain, cgain, cbias)):
-                    nc.scalar.dma_start(
-                        out=vector_rows[GROUPS * i : GROUPS * i + GROUPS, :],
-                        in_=vector.rearrange("(g c) -> g c", g=GROUPS),
-                    )
+                    nc.scalar.dma_start(out=vector_rows[i : i + 1, :], in_=vector.rearrange("(o n) -> o n", o=1))
                 nc.scalar.dma_start(out=sample_row[0:1, :], in_=sweight.rearrange("(o m) -> o m", o=1))
                 load(w_raw, 0, w_view)
                 load(x_raw, 0, x_view, pieces=2)
@@ -248,13 +245,15 @@ def tile_minibatch_discriminator_features_f6_kernel(
                 sweight_all = const.tile([P, M], BF16, name="sweight_all")
 
                 def feature_columns():
-                    turned = bank([P, 2, P])
-                    transpose_word_pairs(turned, vector_rows[:].bitcast(F32))
-                    values = turned[:].rearrange("p u r -> p (u r)").bitcast(BF16)
-                    values = values.rearrange("p (u r e) -> p r u e", u=2, e=2)
-                    nc.vector.tensor_copy(
-                        out=columns[:].rearrange("p i g (u e) -> p (i g) u e", u=2), in_=values[:, 0 : 4 * GROUPS]
-                    )
+                    words = vector_rows[:].bitcast(F32)
+                    for g in range(GROUPS):
+                        turned = bank([P, 2, P])
+                        transpose_word_pairs(turned, words[:, 256 * g : 256 * g + 256])
+                        values = turned[:].rearrange("p u r -> p (u r)").bitcast(BF16)
+                        values = values.rearrange("p (u r e) -> p r u e", u=2, e=2)
+                        nc.vector.tensor_copy(
+                            out=columns[:, :, g].rearrange("p i (u e) -> p i u e", u=2), in_=values[:, 0:4]
+                        )
                     nc.vector.tensor_scalar(out=b_slope[:], in0=b_col, scalar1=SLOPE, scalar2=None, op0=ALU.mult)
 
                 def spread_sweight():
@@ -430,9 +429,9 @@ def tile_minibatch_discriminator_features_f6_kernel(
 
                 w_interleave(0)
                 x_transposes(0)
-                feature_columns()
                 x_quant(0)
                 w_quant(0)
+                feature_columns()
                 spread_sweight()
                 z_matmul(0)
                 z_matmul(1)

from contextlib import ExitStack

import concourse.mybir as mybir
from concourse.masks import make_identity

M, K, N = 1024, 512, 1536
FLOPS = 2 * M * N * (K + N + M)

F32 = mybir.dt.float32
BF16 = mybir.dt.bfloat16
U32 = mybir.dt.uint32
U8 = mybir.dt.uint8
FP8 = mybir.dt.float8_e4m3fn
FP8X4 = mybir.dt.float8_e4m3fn_x4
ALU = mybir.AluOpType
ACT = mybir.ActivationFunctionType

SLOPE = 0.2
P = 128
PACK = 4
PASS = P * PACK
BANK = 512
GROUPS = N // PASS
HALVES = M // PASS
UNITS = GROUPS * HALVES
TILES = UNITS * PACK
ROW_TILES = M // P
P_PIECES = GROUPS * (N // BANK)

INTERLEAVE_ON_SCALAR = (0, 2)
ABS_ON_VECTOR = 768

W_SLOTS = (0, 2)
W_QUANT_LAG = 5
Q_SLOTS = (0, 15)
Q_HALF_STEPS = (5, 0)
Q_QUANT_LAG = 6
P_SLOTS = (0, 3, 6, 7, 13, 17, 18, 23, 23)
P_INTERLEAVE_LAG = 2
P_QUANT_LAG = 5
C_SLOTS = (21, 26)
C_HALF_STEPS = (1, 3)
C_COPY_LAG = 3
A_SLOT = 37


def woven_work():
    entries = []

    def put(slot, what, *args):
        entries.append((slot, len(entries), what, args))

    put(0, "x transposes", 1)
    put(1, "x quant", 1)
    for i, slot in enumerate(W_SLOTS):
        put(slot, "w interleave", i + 1)
        put(slot + W_QUANT_LAG, "w quant", i + 1)
    for k in range(UNITS):
        s = 4 * k
        put(s + 5, "h transposes", k, 0)
        put(s + 7, "h copy", k, 0)
        put(s + 12, "h interleave", k)
        put(s + 5, "h transposes", k, 1)
        put(s + 14, "h quant features", k)
        put(s + 7, "h copy", k, 1)
        put(s + 11, "h quant samples", k)
    for m in range(HALVES):
        for r in range(4):
            slot = Q_SLOTS[m] + Q_HALF_STEPS[m] * r // 2
            put(slot, "q transposes", m, r)
            put(slot + 1, "q copy", m, r)
        put(slot + 1 + Q_QUANT_LAG, "q quant", m)
    for i, slot in enumerate(P_SLOTS):
        put(slot, "p widen", i, 0)
        put(slot + 1, "p widen", i, 2)
        put(slot + P_INTERLEAVE_LAG, "p interleave", i)
        put(slot + P_INTERLEAVE_LAG + P_QUANT_LAG, "p quant", i)
    for g in range(2):
        for j in range(8):
            slot = C_SLOTS[g] + C_HALF_STEPS[g] * j // 2
            put(slot, "c matmuls", g, j // 4, j % 4)
            put(slot + C_COPY_LAG, "c copy", g, j // 4, j % 4)
    for n in range(3):
        put(A_SLOT, "a matmuls", 0, n)
        put(A_SLOT, "a squares", 0, n)
    put(A_SLOT, "a norm", 0)

    work = {}
    for slot, order, what, args in sorted(entries, key=lambda e: (e[0], e[1])):
        work.setdefault(slot, []).append((what, args))
    return work


def tile_minibatch_discriminator_features_f6_kernel(
    tc, x, w, b, fgain, sweight, p_bytes, p_scale, q, pgain, cgain, cbias, own_out, close_out
):
    nc = tc.nc
    with ExitStack() as ctx:
        const = ctx.enter_context(tc.tile_pool(name="const", bufs=1))
        codes = ctx.enter_context(tc.tile_pool(name="codes", bufs=1))
        grouped_pool = ctx.enter_context(tc.tile_pool(name="grouped", bufs=5))
        wide_pool = ctx.enter_context(tc.tile_pool(name="wide", bufs=2))
        h_pool = ctx.enter_context(tc.tile_pool(name="h", bufs=3))
        leaky_pool = ctx.enter_context(tc.tile_pool(name="leaky", bufs=3))
        norm_pool = ctx.enter_context(tc.tile_pool(name="norm", bufs=4))
        context_pool = ctx.enter_context(tc.tile_pool(name="context", bufs=1))
        psum = ctx.enter_context(tc.psum_pool(name="psum", bufs=8))

        ident = const.tile([P, P], F32, name="ident")
        make_identity(nc, ident[:])

        def bank(shape):
            return psum.tile(shape, F32, name="bank", tag="bank")

        def grouped_tile():
            return grouped_pool.tile([P, PASS, PACK], BF16, name="grouped", tag="grouped", align_bytes=64)

        def flat(tile):
            return tile[:].rearrange("p c t -> p (c t)")

        def operand(name, width):
            words = codes.tile([P, width], U32, name=name + "_codes", align_bytes=64)
            scales = codes.tile([P, width], U8, name=name + "_scales", align_bytes=64)
            return words, scales

        def quantize(op, column, grouped):
            cols = slice(column, column + PASS)
            nc.vector.quantize_mx(out=op[0][:, cols].bitcast(FP8X4), scales=op[1][:, cols], in_=grouped)

        def multiply(out, stationary, column, moving, moving_column, start, stop):
            lhs = slice(column, column + P)
            rhs = slice(moving_column, moving_column + BANK)
            nc.tensor.matmul_mx(
                out=out,
                lhsT=stationary[0][:, lhs].bitcast(FP8X4),
                lhsT_scale=stationary[1][:, lhs],
                rhs=moving[0][:, rhs].bitcast(FP8X4),
                rhs_scale=moving[1][:, rhs],
                start=start,
                stop=stop,
            )

        def transpose_word_pairs(out, words):
            for u in range(2):
                nc.tensor.transpose(out[:, u, :], words[:, u::2], ident[:])

        def words_of(grouped, blocks):
            return flat(grouped).bitcast(F32).rearrange("p (b c u) -> p b c u", b=blocks, u=2)

        def interleave(copy, dst, src):
            copy(
                out=dst[:].rearrange("p (c i) t -> p c t i", i=4), in_=src[:].rearrange("p t (c i) -> p c t i", i=4)
            )

        x_mx = [operand("x%d" % m, PASS) for m in range(HALVES)]
        w_mx = [operand("w%d" % g, PASS) for g in range(GROUPS)]
        hf_mx = [operand("hf%d" % g, M) for g in range(GROUPS)]
        hs_mx = [operand("hs%d" % m, N) for m in range(HALVES)]
        q_mx = [operand("q%d" % m, M) for m in range(HALVES)]
        p_mx = [operand("p%d" % g, N) for g in range(GROUPS)]

        with tc.manual_schedule():
            with tc.tile_pool(name="raw", bufs=1) as raw, tc.tile_pool(name="raw_ring", bufs=6) as raw_ring:
                warm = const.tile([P, 1], F32, name="warm")
                minus_half = const.tile([P, 1], F32, name="minus_half")
                vector_rows = raw.tile([P, N], BF16, name="vector_rows")
                sample_row = raw.tile([P, M], BF16, name="sample_row")
                ones = const.tile([P, P], BF16, name="ones")
                nc.vector.memset(vector_rows[:], 0.0)
                nc.vector.memset(sample_row[:], 0.0)
                nc.vector.memset(warm[:], 0.0)
                nc.vector.memset(ones[:], 1.0)
                nc.vector.memset(minus_half[:], -0.5)

                p_raw = [raw.tile([P, PACK, N], U8, name="p_raw%d" % g) for g in range(GROUPS)]
                p_scales = const.tile([P, GROUPS, PACK], F32, name="p_scales")
                pgain_all = const.tile([P, N], BF16, name="pgain_all")
                x_raw, w_raw, q_raw = {}, {}, {}
                x_view = x.rearrange("(m r p) k -> m p r k", p=P, r=4)
                w_view = w.rearrange("(p j) (g c) -> g p j c", j=PACK, g=GROUPS)
                q_view = q.rearrange("(s r p) k -> s p r k", p=P, r=2)
                p_view = p_bytes.rearrange("(g p t) n -> g p t n", p=P, t=PACK)

                def load(store, key, view, pieces=1):
                    shape = [P, 2, M] if store is q_raw else [P, 4, PASS]
                    store[key] = raw_ring.tile(shape, BF16, name="raw_ring", tag="raw_ring")
                    step = shape[1] // pieces
                    for i in range(0, shape[1], step):
                        nc.sync.dma_start(out=store[key][:, i : i + step], in_=view[key][:, i : i + step])

                def load_p(g):
                    for t in (0, 2):
                        nc.sync.dma_start(out=p_raw[g][:, t : t + 2, :], in_=p_view[g][:, t : t + 2, :])

                for i, vector in enumerate((b, fgain, cgain, cbias)):
                    nc.scalar.dma_start(out=vector_rows[i : i + 1, :], in_=vector.rearrange("(o n) -> o n", o=1))
                nc.scalar.dma_start(out=sample_row[0:1, :], in_=sweight.rearrange("(o m) -> o m", o=1))
                load(w_raw, 0, w_view)
                load(x_raw, 0, x_view, pieces=2)
                load(x_raw, 1, x_view)
                nc.sync.dma_start(out=p_scales[:], in_=p_scale.rearrange("(g p t) o -> p g (t o)", p=P, t=PACK))
                load_p(0)
                load(w_raw, 1, w_view)
                load(q_raw, 0, q_view)
                load(q_raw, 1, q_view)
                load(w_raw, 2, w_view)
                load_p(1)
                load(q_raw, 2, q_view)
                load(q_raw, 3, q_view)
                load_p(2)
                nc.sync.dma_start(out=pgain_all[:], in_=pgain.partition_broadcast(P))

                nc.scalar.activation(out=warm[:], in_=warm[:], func=ACT.Exp)

                x_grouped, w_grouped = {}, {}

                def x_transposes(m):
                    x_grouped[m] = grouped_tile()
                    words = words_of(x_grouped[m], 4)
                    for i, copy in enumerate((nc.vector.tensor_copy, nc.scalar.copy)):
                        turned = bank([P, 2, 2, P])
                        for r in range(2):
                            transpose_word_pairs(turned[:, r], x_raw[m][:, 2 * i + r, :].bitcast(F32))
                        copy(out=words[:, 2 * i : 2 * i + 2], in_=turned[:].rearrange("p r u c -> p r c u"))

                def x_quant(m):
                    quantize(x_mx[m], 0, flat(x_grouped[m]))

                def w_interleave(g):
                    w_grouped[g] = grouped_tile()
                    dst = w_grouped[g][:].rearrange("p (t j) k -> p j k t", t=PACK)
                    src = w_raw[g][:].rearrange("p k (j t) -> p j k t", t=PACK)
                    if g == 0:
                        nc.vector.tensor_copy(out=dst[:, :, :, 0:2], in_=src[:, :, :, 0:2])
                        nc.scalar.copy(out=dst[:, :, :, 2:4], in_=src[:, :, :, 2:4])
                    else:
                        nc.vector.tensor_copy(out=dst, in_=src)

                def w_quant(g):
                    quantize(w_mx[g], 0, flat(w_grouped[g]))

                columns = const.tile([P, 4, GROUPS, PACK], F32, name="columns")
                b_slope = const.tile([P, GROUPS, PACK], F32, name="b_slope")
                b_col, fgain_col, cgain_col, cbias_col = (columns[:, i] for i in range(4))
                sweight_all = const.tile([P, M], BF16, name="sweight_all")

                def feature_columns():
                    words = vector_rows[:].bitcast(F32)
                    for g in range(GROUPS):
                        turned = bank([P, 2, P])
                        transpose_word_pairs(turned, words[:, 256 * g : 256 * g + 256])
                        values = turned[:].rearrange("p u r -> p (u r)").bitcast(BF16)
                        values = values.rearrange("p (u r e) -> p r u e", u=2, e=2)
                        nc.vector.tensor_copy(
                            out=columns[:, :, g].rearrange("p i (u e) -> p i u e", u=2), in_=values[:, 0:4]
                        )
                    nc.vector.tensor_scalar(out=b_slope[:], in0=b_col, scalar1=SLOPE, scalar2=None, op0=ALU.mult)

                def spread_sweight():
                    for m0 in range(0, M, BANK):
                        spread = bank([P, BANK])
                        nc.tensor.matmul(
                            spread[:], lhsT=ones[:], rhs=sample_row[:, m0 : m0 + BANK], start=True, stop=True
                        )
                        nc.scalar.copy(out=sweight_all[:, m0 : m0 + BANK], in_=spread[:])

                z_bank, lower, leaky, h_tile = {}, {}, {}, {}

                def z_matmul(s):
                    k, t = divmod(s, PACK)
                    z_bank[s] = bank([P, BANK])
                    multiply(z_bank[s][:], w_mx[k // 2], P * t, x_mx[k % 2], 0, True, True)

                def leaky_lower(s):
                    k, t = divmod(s, PACK)
                    lower[s] = leaky_pool.tile([P, BANK], F32, name="lower", tag="lower")
                    nc.scalar.activation(
                        out=lower[s][:],
                        in_=z_bank[s][:],
                        func=ACT.Identity,
                        scale=SLOPE,
                        bias=b_slope[:, k // 2, t : t + 1],
                    )

                def leaky_max(s):
                    k, t = divmod(s, PACK)
                    leaky[s] = leaky_pool.tile([P, BANK], F32, name="leaky", tag="leaky")
                    nc.vector.scalar_tensor_tensor(
                        out=leaky[s][:],
                        in0=z_bank[s][:],
                        scalar=b_col[:, k // 2, t : t + 1],
                        in1=lower[s][:],
                        op0=ALU.add,
                        op1=ALU.max,
                    )

                def gains(s):
                    k, t = divmod(s, PACK)
                    if t == 0:
                        h_tile[k] = h_pool.tile([P, PACK, BANK], BF16, name="h", tag="h")
                    m0 = BANK * (k % 2)
                    nc.vector.scalar_tensor_tensor(
                        out=h_tile[k][:, t, :],
                        in0=leaky[s][:],
                        scalar=fgain_col[:, k // 2, t : t + 1],
                        in1=sweight_all[:, m0 : m0 + BANK],
                        op0=ALU.mult,
                        op1=ALU.mult,
                    )

                hf_grouped = {}

                def h_interleave(k):
                    hf_grouped[k] = grouped_tile()
                    copy = nc.scalar.copy if k in INTERLEAVE_ON_SCALAR else nc.vector.tensor_copy
                    interleave(copy, hf_grouped[k], h_tile[k])

                def h_quant_features(k):
                    quantize(hf_mx[k // 2], PASS * (k % 2), flat(hf_grouped[k]))

                h_turned, hs_grouped = {}, {}

                def h_transposes(k, i):
                    h_turned[(k, i)] = bank([P, 2, 2, P])
                    for t in range(2):
                        transpose_word_pairs(h_turned[(k, i)][:, t], h_tile[k][:, 2 * i + t, :].bitcast(F32))

                def h_copy(k, i):
                    if i == 0:
                        hs_grouped[k] = grouped_tile()
                    nc.scalar.copy(
                        out=words_of(hs_grouped[k], 4)[:, 2 * i : 2 * i + 2],
                        in_=h_turned[(k, i)][:].rearrange("p t u c -> p t c u"),
                    )

                def h_quant_samples(k):
                    quantize(hs_mx[k % 2], PASS * (k // 2), flat(hs_grouped[k]))

                q_turned, q_grouped = {}, {}

                def q_transposes(m, r):
                    q_turned[(m, r)] = bank([P, 2, 2, P])
                    words = q_raw[2 * m + r // 2][:, r % 2, :].bitcast(F32)
                    for c in range(HALVES):
                        transpose_word_pairs(q_turned[(m, r)][:, c], words[:, 256 * c : 256 * c + 256])

                def q_copy(m, r):
                    if r == 0:
                        q_grouped[m] = raw.tile(
                            [P, HALVES, PASS, PACK], BF16, name="q_grouped", tag="q_grouped", align_bytes=64
                        )
                    words = q_grouped[m][:].rearrange("p c s t -> p (c s t)").bitcast(F32)
                    words = words.rearrange("p (c r s u) -> p c r s u", c=HALVES, r=4, u=2)
                    nc.scalar.copy(out=words[:, :, r], in_=q_turned[(m, r)][:].rearrange("p c u s -> p c s u"))

                def q_quant(m):
                    for c in range(HALVES):
                        quantize(q_mx[c], PASS * m, q_grouped[m][:, c].rearrange("p s t -> p (s t)"))

                p_wide, p_grouped = {}, {}

                def p_widen(i, first):
                    g, n = divmod(i, 3)
                    if first == 0:
                        p_wide[i] = wide_pool.tile([P, PACK, BANK], BF16, name="wide", tag="wide")
                    for t in (first, first + 1):
                        nc.scalar.activation(
                            out=p_wide[i][:, t, :],
                            in_=p_raw[g][:, t, BANK * n : BANK * n + BANK].bitcast(FP8),
                            func=ACT.Copy,
                            scale=p_scales[:, g, t : t + 1],
                        )

                def p_interleave(i):
                    p_grouped[i] = grouped_tile()
                    interleave(nc.vector.tensor_copy, p_grouped[i], p_wide[i])

                def p_quant(i):
                    g, n = divmod(i, 3)
                    quantize(p_mx[g], PASS * n, flat(p_grouped[i]))

                c_bank, context = {}, {}

                def c_matmuls(g, m, t):
                    c_bank[(g, m, t)] = bank([P, BANK])
                    for c in range(HALVES):
                        multiply(
                            c_bank[(g, m, t)][:], hs_mx[c], PASS * g + P * t, q_mx[c], BANK * m, c == 0, c == HALVES - 1
                        )

                def c_copy(g, m, t, pool=context_pool):
                    if t == 0:
                        context[(g, m)] = pool.tile([P, PACK, BANK], F32, name="context%d%d" % (g, m))
                    nc.scalar.activation(
                        out=context[(g, m)][:, t, :],
                        in_=c_bank[(g, m, t)][:],
                        func=ACT.Identity,
                        scale=cgain_col[:, g, t : t + 1],
                        bias=cbias_col[:, g, t : t + 1],
                    )

                a_bank, squares, inverse = {}, {}, {}

                def a_matmuls(r, n):
                    a_bank[(r, n)] = bank([P, BANK])
                    for g in range(GROUPS):
                        multiply(a_bank[(r, n)][:], hf_mx[g], P * r, p_mx[g], BANK * n, g == 0, g == GROUPS - 1)

                def a_squares(r, n):
                    if n == 0:
                        squares[r] = norm_pool.tile([P, 3], F32, name="squares", tag="squares")
                    unused = norm_pool.tile([P, BANK], BF16, name="unused", tag="unused")
                    nc.scalar.activation(
                        out=unused[:],
                        in_=a_bank[(r, n)][:],
                        func=ACT.Square,
                        scale=1.0 / N**0.5,
                        accum_out=squares[r][:, n : n + 1],
                    )

                def a_norm(r):
                    mean = norm_pool.tile([P, 1], F32, name="mean", tag="mean")
                    inverse[r] = norm_pool.tile([P, 1], F32, name="inverse", tag="inverse")
                    parts = squares[r]
                    nc.gpsimd.tensor_scalar(
                        out=mean[:], in0=parts[:, 0:1], scalar1=parts[:, 1:2], scalar2=parts[:, 2:3], op0=ALU.add, op1=ALU.add
                    )
                    nc.gpsimd.tensor_tensor(out=inverse[r][:], in0=mean[:], in1=minus_half[:], op=ALU.pow)

                w_interleave(0)
                x_transposes(0)
                x_quant(0)
                w_quant(0)
                feature_columns()
                spread_sweight()
                z_matmul(0)
                z_matmul(1)
                leaky_lower(0)

                does = {
                    "x transposes": x_transposes,
                    "x quant": x_quant,
                    "w interleave": w_interleave,
                    "w quant": w_quant,
                    "h transposes": h_transposes,
                    "h copy": h_copy,
                    "h quant samples": h_quant_samples,
                    "h interleave": h_interleave,
                    "h quant features": h_quant_features,
                    "q transposes": q_transposes,
                    "q copy": q_copy,
                    "q quant": q_quant,
                    "p widen": p_widen,
                    "p interleave": p_interleave,
                    "p quant": p_quant,
                    "c matmuls": c_matmuls,
                    "c copy": c_copy,
                    "a matmuls": a_matmuls,
                    "a squares": a_squares,
                    "a norm": a_norm,
                }
                work = woven_work()
                for s in range(max(work) + 1):
                    if s + 2 < TILES:
                        z_matmul(s + 2)
                    if s + 1 < TILES:
                        leaky_lower(s + 1)
                    if s < TILES:
                        leaky_max(s)
                    here = work.get(s, [])
                    for what, args in here[: len(here) // 2]:
                        does[what](*args)
                    if 0 < s <= TILES:
                        gains(s - 1)
                    for what, args in here[len(here) // 2 :]:
                        does[what](*args)

            with (
                tc.tile_pool(name="context_last", bufs=1) as context_last,
                tc.tile_pool(name="own", bufs=4) as own_pool,
                tc.tile_pool(name="difference", bufs=3) as difference_pool,
            ):
                own_view = own_out.rearrange("(r p) n -> r p n", p=P)
                close_view = close_out.rearrange("(r p) n -> r p n", p=P)
                own, difference, context_bank = {}, {}, {}

                def own_columns(r, n):
                    if n == 0:
                        own[r] = own_pool.tile([P, N], F32, name="own", tag="own")
                    cols = slice(BANK * n, BANK * n + BANK)
                    nc.vector.scalar_tensor_tensor(
                        out=own[r][:, cols],
                        in0=a_bank[(r, n)][:],
                        scalar=inverse[r][:],
                        in1=pgain_all[:, cols],
                        op0=ALU.mult,
                        op1=ALU.mult,
                    )

                def own_rows(r):
                    for n in range(3):
                        own_columns(r, n)
                    nc.sync.dma_start(out=own_view[r], in_=own[r][:])

                def a_rows(r):
                    for n in range(3):
                        a_matmuls(r, n)
                        a_squares(r, n)
                    a_norm(r)

                def context_transposes(r, g):
                    context_bank[(r, g)] = bank([P, PACK, P])
                    m, c0 = r // 4, P * (r % 4)
                    for t in range(PACK):
                        nc.tensor.transpose(
                            context_bank[(r, g)][:, t, :], context[(g, m)][:, t, c0 : c0 + P], ident[:]
                        )

                def subtract_context(r, g):
                    if g == 0:
                        difference[r] = difference_pool.tile([P, N], F32, name="difference", tag="difference")
                    cols = slice(PASS * g, PASS * g + PASS)
                    nc.vector.tensor_tensor(
                        out=difference[r][:, cols].rearrange("p (j t) -> p j t", t=PACK),
                        in0=own[r][:, cols].rearrange("p (j t) -> p j t", t=PACK),
                        in1=context_bank[(r, g)][:].rearrange("p t j -> p j t"),
                        op=ALU.subtract,
                    )

                def absolute_on_vector(r, lo, hi):
                    d = difference[r][:, lo:hi]
                    nc.vector.scalar_tensor_tensor(out=d, in0=d, scalar=-1.0, in1=d, op0=ALU.mult, op1=ALU.max)

                def absolute_on_scalar(r, lo, hi):
                    d = difference[r][:, lo:hi]
                    nc.scalar.activation(out=d, in_=d, func=ACT.Abs)

                def closeness(r, lo, hi):
                    d = difference[r][:, lo:hi]
                    nc.scalar.activation(out=d, in_=d, func=ACT.Exp, scale=-1.0)
                    nc.sync.dma_start(out=close_view[r][:, lo:hi], in_=d)

                def last_context(m, t):
                    c_matmuls(GROUPS - 1, m, t)
                    c_copy(GROUPS - 1, m, t, context_last)

                for t in range(PACK):
                    last_context(0, t)
                a_rows(1)
                own_rows(0)
                for r in range(ROW_TILES):
                    for g in range(GROUPS):
                        context_transposes(r, g)
                    for g in range(GROUPS):
                        subtract_context(r, g)
                    if r < 2:
                        last_context(1, r)
                    elif r == 2:
                        last_context(1, 2)
                        last_context(1, 3)
                    if r + 1 < ROW_TILES:
                        own_rows(r + 1)
                        absolute_on_scalar(r, ABS_ON_VECTOR, N)
                        if r + 2 < ROW_TILES:
                            a_rows(r + 2)
                        absolute_on_vector(r, 0, ABS_ON_VECTOR)
                        closeness(r, 0, N)
                    else:
                        for n in range(3):
                            absolute_on_vector(r, BANK * n, BANK * n + BANK)
                            closeness(r, BANK * n, BANK * n + BANK)
